import numpy as np
import ml_dtypes


def mxq(x, axis, fmt="e4m3"):
    dtype, down = {"e4m3": (ml_dtypes.float8_e4m3fn, 7), "e5m2": (ml_dtypes.float8_e5m2, 14)}[fmt]
    v = np.moveaxis(np.asarray(x, np.float32).astype(ml_dtypes.bfloat16).astype(np.float64), axis, -1)
    blocks = v.reshape(v.shape[:-1] + (-1, 32))
    amax = np.abs(blocks).max(-1, keepdims=True)
    byte = np.maximum(np.where(amax > 0, np.frexp(amax)[1] - 1 + 127, 0) - down, 1)
    scale = np.exp2(byte - 127.0)
    codes = (blocks / scale).astype(np.float32).astype(dtype).astype(np.float64)
    return np.moveaxis((codes * scale).reshape(v.shape), -1, axis)


WIDE = False


def mx_kscale(k):
    if not WIDE:
        return np.ones(k)
    levels = np.array([10, -10, 5, -5, 0])
    if k % 512:
        return np.exp2(np.random.permutation(np.resize(levels, k // 32))).repeat(32)
    a = np.empty((k // 512, 16))
    for p in range(k // 512):
        a[p, :8] = np.random.permutation(np.resize(levels, 8))
        for g in range(8):
            far = levels[np.abs(levels - a[p, g]) >= 10]
            a[p, g + 8] = far[np.random.randint(len(far))]
    return np.exp2(a.ravel()).repeat(32)


def f64(x):
    return np.asarray(x).astype(np.float64)


def striped(idx):
    return np.tile(idx.reshape(-1, 16).T, (8, 1)).astype(np.uint16)


def unstriped(offs):
    return offs[:16].T.reshape(-1).astype(np.int64)


E2M1 = np.array([0.0, 0.5, 1.0, 1.5, 2.0, 3.0, 4.0, 6.0, -0.0, -0.5, -1.0, -1.5, -2.0, -3.0, -4.0, -6.0])


def pack_weight(w, fmt):
    k, n = w.shape
    w = f64(np.asarray(w, np.float32).astype(ml_dtypes.bfloat16)).reshape(k // 32, 32, n)
    amax = np.abs(w).max(1)
    if fmt == "e4m3":
        byte = np.frexp(amax)[1] - 1 + 127 - 7
    else:
        mant, ex = np.frexp(amax / 6.0)
        byte = np.where(mant > 0.5, ex, ex - 1) + 127
    byte = np.clip(np.where(amax > 0, byte, 1), 1, 254)
    scaled = (w * np.exp2(127.0 - byte)[:, None, :]).reshape(k, n).astype(np.float32)
    by_word = np.ascontiguousarray(scaled.reshape(k // 512, 128, 4, n).transpose(0, 1, 3, 2))
    if fmt == "e4m3":
        words = by_word.astype(ml_dtypes.float8_e4m3fn).view(np.uint8)
    else:
        c = by_word.astype(ml_dtypes.float4_e2m1fn).view(np.uint8) & 0xF
        words = (c[..., 0::2] | (c[..., 1::2] << 4)).reshape(k // 512, 128, 2 * n)
    return np.ascontiguousarray(words), np.ascontiguousarray(byte.astype(np.uint8).reshape(k // 512, 16, n))


def unpack_weight(words, scales, fmt):
    g, _, n = scales.shape
    words = np.ascontiguousarray(words).reshape(g, 128, n, -1)
    if fmt == "e4m3":
        vals = words.view(ml_dtypes.float8_e4m3fn).astype(np.float64)
    else:
        nib = np.empty((g, 128, n, 4), np.uint8)
        nib[..., 0::2] = words & 0xF
        nib[..., 1::2] = words >> 4
        vals = E2M1[nib]
    vals = vals * np.repeat(np.exp2(scales.astype(np.float64) - 127.0), 8, axis=1)[..., None]
    return vals.transpose(0, 1, 3, 2).reshape(g * 512, n)


def gelu(v):
    return 0.5 * v * (1.0 + np.tanh(np.sqrt(2.0 / np.pi) * (v + 0.044715 * v**3)))


K, H, T, S, T2, P = 1024, 1536, 2048, 512, 1024, 512

def setup_inputs():
    n = np.random.standard_normal
    s = mx_kscale(K)[:, None]
    u = mx_kscale(H)[:, None]
    d = {}
    d["tab_words"], d["tab_scales"] = pack_weight(n((K, T)) * s, "e4m3")
    d["w4_words"], d["w4_scales"] = pack_weight(n((K, H)) / s * u.T / (2 * K) ** 0.5, "e2m1")
    d["w1"] = (n((K, H)) / s * u.T / (2 * K) ** 0.5).astype(np.float32)
    d["lim"] = (np.random.uniform(0.2, 1.5, (H, S)) * u).astype(np.float32)
    d["wgs"] = np.exp(0.3 * n((128, S))).astype(np.float32)
    d["page0"] = (n((H, T2)) * u).astype(np.float32)
    d["cen"] = (0.7 * n(H) * u[:, 0]).astype(np.float32)
    d["cap"] = ((0.3 + 0.5 * n(H)) * u[:, 0]).astype(np.float32)
    d["vec"] = (n(H) / u[:, 0] ** 2 / H ** 0.5).astype(np.float32)
    d["due"] = (0.8 * n((T2, P))).astype(np.float32)
    d["offs"] = striped(np.random.permutation(T)[:S])
    d["offs2"] = striped(np.random.permutation(T2)[:S])
    d["offs3"] = striped(np.random.permutation(T2)[:P])
    return d

def reference(tab_words, tab_scales, w4_words, w4_scales, w1, lim, wgs, page0, cen, cap, vec, due, offs, offs2, offs3):
    v = unpack_weight(tab_words, tab_scales, "e4m3")[:, unstriped(offs)]
    w4 = unpack_weight(w4_words, w4_scales, "e2m1")
    a = w4.T @ v + mxq(f64(w1), 0, "e4m3").T @ v
    h = np.minimum(np.abs(a), f64(lim)) + a
    page = f64(page0).copy()
    page[:, unstriped(offs2)] = np.tile(f64(wgs), (H // 128, 1)) * h
    x = np.minimum(page[:, unstriped(offs3)] - f64(cen)[:, None], f64(cap)[:, None]) * f64(vec)[:, None]
    e = mxq(page, 0, "e4m3").T @ mxq(x, 0, "e4m3")
    y = e - f64(due)
    return y / (1.0 + np.exp(-y))

@@ -1,0 +1,415 @@
+from contextlib import ExitStack
+
+import concourse.mybir as mybir
+from concourse.masks import make_identity
+
+K, H, T, S, T2, NP = 1024, 1536, 2048, 512, 1024, 512
+FLOPS = 2 * (2 * K * H * S + H * T2 * NP)
+
+F32 = mybir.dt.float32
+BF16 = mybir.dt.bfloat16
+I32 = mybir.dt.int32
+U32 = mybir.dt.uint32
+U16 = mybir.dt.uint16
+U8 = mybir.dt.uint8
+FP8X4 = mybir.dt.float8_e4m3fn_x4
+FP4X4 = mybir.dt.float4_e2m1fn_x4
+ALU = mybir.AluOpType
+ACT = mybir.ActivationFunctionType
+
+P = 128
+PACK = 4
+KP = P * PACK
+A_PASSES = K // KP
+R_PASSES = H // KP
+TILES = R_PASSES * PACK
+M_TILES = T2 // P
+QUAD = 32
+AHEAD = 2
+PAGE_AHEAD = 3
+RING_BANKS = 4
+
+
+def tile_list_vanilla_page_scores_kernel(
+    tc, tab_words, tab_scales, w4_words, w4_scales, w1, lim, wgs, page0, cen, cap, vec, due, offs, offs2, offs3, out
+):
+    nc = tc.nc
+    with ExitStack() as ctx:
+        lists = ctx.enter_context(tc.tile_pool(name="lists", bufs=1))
+        keep = ctx.enter_context(tc.tile_pool(name="keep", bufs=1))
+        ring = ctx.enter_context(tc.tile_pool(name="ring", bufs=2))
+        psum = ctx.enter_context(tc.psum_pool(name="psum", bufs=1))
+
+        def bank(i, shape):
+            return psum.tile(shape, F32, name="bank%d" % i, tag="bank%d" % i)
+
+        idx1 = lists.tile([P, S // 16], U16)
+        idx2 = lists.tile([P, S // 16], U16)
+        idx3 = lists.tile([P, NP // 16], U16)
+        nc.sync.dma_start(idx1[:], offs)
+        nc.sync.dma_start(idx2[:], offs2)
+        nc.sync.dma_start(idx3[:], offs3)
+        row_consts = []
+        for name, v in (("cen", cen), ("cap", cap), ("vec", vec)):
+            cols = keep.tile([P, R_PASSES, PACK], F32, name=name)
+            nc.sync.dma_start(out=cols[:], in_=v.rearrange("(b p t) -> p b t", p=P, t=PACK))
+            row_consts.append(cols)
+        cen_c, cap_c, vec_c = row_consts
+        w4_raw = keep.tile([P, A_PASSES, 2 * H], U8, align_bytes=64)
+        nc.sync.dma_start(out=w4_raw[:].bitcast(I32), in_=w4_words.rearrange("a p n -> p a n").bitcast(I32))
+        tab_sc = keep.tile([P, A_PASSES, T], U8, align_bytes=64)
+        w4_sc = keep.tile([P, A_PASSES, H], U8, align_bytes=64)
+        nc.vector.memset(w4_sc[:].rearrange("p a n -> p (a n)").bitcast(I32), 0)
+        nc.vector.memset(tab_sc[:].rearrange("p a n -> p (a n)").bitcast(I32), 0)
+        ident = keep.tile([P, P], F32)
+        make_identity(nc, ident[:])
+        warm = keep.tile([P, 1], F32)
+        nc.scalar.activation(out=warm[:], in_=ident[:, 0:1], func=ACT.Silu)
+
+        tab = []
+
+        def load_tab(a):
+            words = ring.tile([P, T], I32, name="tab", tag="staged", align_bytes=64)
+            nc.sync.dma_start(out=words[:], in_=tab_words[a].rearrange("p n i -> p (n i)").bitcast(I32))
+            tab.append(words)
+
+        def load_scale_rows(plane, rows, q):
+            nc.sync.dma_start(
+                out=plane[QUAD * q : QUAD * q + 4, :, :].bitcast(I32),
+                in_=rows[:, 4 * q : 4 * q + 4, :].rearrange("a q n -> q a n").bitcast(I32),
+            )
+
+        w1_raw = {}
+
+        def load_w1(b, a):
+            raw = ring.tile([P, PACK, KP], F32, name="w1_raw")
+            rows = w1[KP * a : KP * (a + 1), KP * b : KP * (b + 1)]
+            nc.sync.dma_start(out=raw[:], in_=rows.rearrange("(p j) c -> p j c", j=PACK))
+            w1_raw[a, b] = raw
+
+        lim_t, page_t = {}, {}
+
+        def rows_of(x, n):
+            b, t = divmod(n, PACK)
+            return x[KP * b : KP * (b + 1), :].rearrange("(p t) c -> p t c", t=PACK)[:, t, :]
+
+        def load_lim(n):
+            lim_t[n] = ring.tile([P, S], F32, name="lim", bufs=4)
+            nc.sync.dma_start(out=lim_t[n][:], in_=rows_of(lim, n))
+
+        def load_page(n):
+            page_t[n] = ring.tile([P, T2], F32, name="page", bufs=6)
+            nc.sync.dma_start(out=page_t[n][:], in_=rows_of(page0, n))
+
+        load_tab(0)
+        for q in (0, 2, 1, 3):
+            load_scale_rows(w4_sc, w4_scales, q)
+        for q in (0, 2):
+            load_scale_rows(tab_sc, tab_scales, q)
+        load_tab(1)
+        load_w1(0, 0)
+        for q in (1, 3):
+            load_scale_rows(tab_sc, tab_scales, q)
+        load_w1(0, 1)
+        load_lim(0)
+        wgs_v = wgs.rearrange("(p t) j -> p t j", t=PACK)
+        wg_first = keep.tile([P, S], F32)
+        for q in range(P // QUAD):
+            nc.sync.dma_start(out=wg_first[QUAD * q : QUAD * (q + 1), :], in_=wgs_v[:, 0, :])
+        load_page(0)
+        load_lim(1)
+        load_w1(1, 0)
+        wg_rest = keep.tile([P, PACK - 1, S], F32)
+        for q in range(P // QUAD):
+            nc.sync.dma_start(out=wg_rest[QUAD * q : QUAD * (q + 1), :, :], in_=wgs_v[:, 1:PACK, :])
+        load_page(1)
+        load_w1(1, 1)
+        load_lim(2)
+        load_page(2)
+        load_lim(3)
+
+        w4_dealt = keep.tile([P, A_PASSES * R_PASSES, PACK, 2 * P], U8, align_bytes=64)
+        nc.vector.tensor_copy(
+            out=w4_dealt[:].bitcast(U16).rearrange("p g t (o i) -> p g o t i", i=8),
+            in_=w4_raw[:].rearrange("p a n -> p (a n)").bitcast(U16).rearrange("p (g o i t) -> p g o t i", o=16, i=8, t=PACK),
+        )
+        w4_sc_dealt = keep.tile([P, A_PASSES * R_PASSES, PACK, P], U8, align_bytes=64)
+        nc.vector.tensor_copy(
+            out=w4_sc_dealt[:].rearrange("p g t (o i) -> p g o t i", i=16),
+            in_=w4_sc[:].rearrange("p a n -> p (a n)").rearrange("p (g o i t) -> p g o t i", o=8, i=16, t=PACK),
+        )
+
+        v_words, v_scales = [], []
+        for a in range(A_PASSES):
+            sc = keep.tile([P, S], U8, name="v_scales%d" % a, align_bytes=64)
+            nc.vector.tensor_copy(out=sc[:], in_=tab_sc[:, a, :].indirect(idx1[:]))
+            v_scales.append(sc)
+        for a in range(A_PASSES):
+            words = keep.tile([P, S], I32, name="v_words%d" % a, align_bytes=64)
+            nc.vector.tensor_copy(out=words[:].bitcast(U32), in_=tab[a][:].bitcast(U32).indirect(idx1[:]))
+            v_words.append(words)
+
+        w1_bf, w1_codes, w1_scales = {}, {}, {}
+
+        def cast_w1(a, b, vector_m):
+            grouped = ring.tile([P, PACK, P, PACK], BF16, name="w1_bf", align_bytes=64)
+            dst = grouped[:].rearrange("p t m j -> p m j t")
+            src = w1_raw[a, b][:].rearrange("p j (m t) -> p m j t", t=PACK)
+            if vector_m > 0:
+                nc.vector.tensor_copy(out=dst[:, 0:vector_m], in_=src[:, 0:vector_m])
+            nc.scalar.copy(out=dst[:, vector_m:P], in_=src[:, vector_m:P])
+            w1_bf[a, b] = grouped
+
+        def quant_w1(a, b):
+            codes = ring.tile([P, KP], U32, name="w1_codes", bufs=4, align_bytes=64)
+            scales = ring.tile([P, KP], U8, name="w1_scales", bufs=4, align_bytes=64)
+            nc.vector.quantize_mx(
+                out=codes[:].bitcast(FP8X4), scales=scales[:], in_=w1_bf[a, b][:].rearrange("p t m j -> p (t m j)")
+            )
+            w1_codes[a, b], w1_scales[a, b] = codes, scales
+
+        def first_product(n):
+            b, t = divmod(n, PACK)
+            acc = bank((n + 2) % RING_BANKS, [P, S])
+            cols = slice(P * t, P * (t + 1))
+            for a in range(A_PASSES):
+                g = R_PASSES * a + b
+                nc.tensor.matmul_mx(
+                    out=acc[:],
+                    lhsT=w4_dealt[:, g, t, :].bitcast(FP4X4),
+                    lhsT_scale=w4_sc_dealt[:, g, t, :],
+                    rhs=v_words[a][:].bitcast(FP8X4),
+                    rhs_scale=v_scales[a][:],
+                    start=(a == 0),
+                    stop=False,
+                )
+            for a in range(A_PASSES):
+                nc.tensor.matmul_mx(
+                    out=acc[:],
+                    lhsT=w1_codes[a, b][:, cols].bitcast(FP8X4),
+                    lhsT_scale=w1_scales[a, b][:, cols],
+                    rhs=v_words[a][:].bitcast(FP8X4),
+                    rhs_scale=v_scales[a][:],
+                    start=False,
+                    stop=(a == A_PASSES - 1),
+                )
+            return acc
+
+        a_sb, half_sum = {}, {}
+
+        turned_t = {}
+
+        def front(n):
+            acc = first_product(n)
+            if n < TILES - 1:
+                a_sb[n] = ring.tile([P, S], F32, name="a_sb")
+            else:
+                a_sb[n] = ring.tile([P, S], F32, name="a_sb_last", tag="late", bufs=1, align_bytes=64)
+            nc.scalar.copy(out=a_sb[n][:], in_=acc[:])
+            turned = bank(RING_BANKS + n % RING_BANKS, [P, S // P, P])
+            for c in range(S // P):
+                cols = slice(P * c, P * (c + 1))
+                nc.tensor.matmul(turned[:, c, :], lim_t[n][:, cols], ident[:], start=True, stop=False, is_transpose=True)
+                nc.tensor.matmul(turned[:, c, :], a_sb[n][:, cols], ident[:], start=False, stop=True, is_transpose=True)
+            turned_t[n] = turned
+
+        def turn_back(n):
+            turned = turned_t[n]
+            turned_sb = ring.tile([P, S // P, P], F32, name="turned_sb", tag="step", bufs=1, align_bytes=64)
+            nc.scalar.activation(out=turned_sb[:], in_=turned[:], func=ACT.Copy, scale=0.5)
+            half_sum[n] = bank(n % RING_BANKS, [P, S // P, P])
+            for c in range(S // P):
+                nc.tensor.transpose(half_sum[n][:, c, :], turned_sb[:, c, :], ident[:])
+
+        wg_first2 = keep.tile([P, S], F32)
+
+        def make_h(n):
+            h = ring.tile([P, S], F32, name="h")
+            if n == 0:
+                acc = first_product(0)
+                relu2 = ring.tile([P, S], F32, name="a_sb")
+                nc.scalar.activation(out=relu2[:], in_=acc[:], func=ACT.Relu, scale=2.0)
+                total = ring.tile([P, S], F32, name="total", tag="step", bufs=1, align_bytes=64)
+                nc.vector.tensor_tensor(out=total[:], in0=acc[:], in1=lim_t[0][:], op=ALU.add)
+                nc.vector.tensor_tensor(out=h[:], in0=total[:], in1=relu2[:], op=ALU.min)
+                return h, wg_first[:]
+            nc.vector.scalar_tensor_tensor(
+                out=h[:],
+                in0=a_sb[n][:],
+                scalar=0.0,
+                in1=half_sum[n][:].rearrange("p c r -> p (c r)"),
+                op0=ALU.max,
+                op1=ALU.min,
+            )
+            t = n % PACK
+            return h, (wg_first2[:] if t == 0 else wg_rest[:, t - 1, :])
+
+        staged, page_bf, x_planes, x_bf, picked = {}, {}, {}, {}, {}
+        last = R_PASSES - 1
+
+        def gather(n):
+            picked[n] = ring.tile([P, NP], F32, name="picked", bufs=1)
+            nc.vector.tensor_copy(out=picked[n][:], in_=page_t[n][:].indirect(idx3[:]))
+
+        def scatter(n, h, weight):
+            b, t = divmod(n, PACK)
+            nc.vector.tensor_tensor(out=page_t[n][:].indirect(idx2[:]), in0=h[:], in1=weight, op=ALU.mult)
+            if n < TILES - 1:
+                if t == 0:
+                    staged[b] = ring.tile([P, PACK, T2], F32, name="staged", align_bytes=64)
+                nc.sync.dma_start(out=staged[b][:, t, :], in_=page_t[n][:])
+
+        def make_x(n):
+            b, t = divmod(n, PACK)
+            if n < TILES - 2:
+                u = ring.tile([P, NP], F32, name="u", tag="step", bufs=1, align_bytes=64)
+            else:
+                u = ring.tile([P, NP], F32, name="u_last", tag="a_sb")
+            nc.vector.tensor_scalar(
+                out=u[:],
+                in0=picked[n][:],
+                scalar1=cen_c[:, b, t : t + 1],
+                scalar2=cap_c[:, b, t : t + 1],
+                op0=ALU.subtract,
+                op1=ALU.min,
+            )
+            factor = vec_c[:, b, t : t + 1]
+            if b < last:
+                if t == 0:
+                    x_planes[b] = ring.tile([P, PACK, NP], BF16, name="x_planes")
+                nc.scalar.activation(out=x_planes[b][:, t, :], in_=u[:], func=ACT.Copy, scale=factor)
+            else:
+                if t == 0:
+                    x_bf[b] = ring.tile([P, NP, PACK], BF16, name="x_last", bufs=1, align_bytes=64)
+                if t < 2:
+                    nc.scalar.activation(out=x_bf[b][:, :, t], in_=u[:], func=ACT.Copy, scale=factor)
+                else:
+                    nc.vector.tensor_scalar(out=x_bf[b][:, :, t], in0=u[:], scalar1=factor, scalar2=None, op0=ALU.mult)
+
+        def weave_x(b):
+            x_bf[b] = ring.tile([P, NP, PACK], BF16, name="x_bf", align_bytes=64)
+            nc.scalar.copy(
+                out=x_bf[b][:].rearrange("p (c i) t -> p c t i", i=4),
+                in_=x_planes[b][:].rearrange("p t (c i) -> p c t i", i=4),
+            )
+
+        x_codes, x_scales, page_codes, page_scales = {}, {}, {}, {}
+
+        def quant_x(b):
+            if b == last - 1:
+                x_codes[b] = ring.tile([P, NP], U32, name="x_codes_late", tag="late", bufs=1, align_bytes=64)
+            else:
+                x_codes[b] = keep.tile([P, NP], U32, name="x_codes%d" % b, align_bytes=64)
+            x_scales[b] = keep.tile([P, NP], U8, name="x_scales%d" % b, align_bytes=64)
+            nc.vector.quantize_mx(
+                out=x_codes[b][:].bitcast(FP8X4), scales=x_scales[b][:], in_=x_bf[b][:].rearrange("p c t -> p (c t)")
+            )
+
+        HALF = T2 // 2
+
+        def weave_page(b, half, planes):
+            if b < last:
+                piece = ring.tile([P, HALF, PACK], BF16, name="page_bf", align_bytes=64)
+                page_bf[b, half] = piece[:]
+            elif half == 0:
+                whole = ring.tile([P, 2, HALF, PACK], BF16, name="page_last", tag="step", bufs=1, align_bytes=64)
+                page_bf[b, 0], page_bf[b, 1] = whole[:, 0], whole[:, 1]
+            src = staged[b][:, 0:planes, HALF * half : HALF * (half + 1)]
+            nc.scalar.copy(
+                out=page_bf[b, half].rearrange("p (c i) t -> p c t i", i=4)[:, :, 0:planes, :],
+                in_=src.rearrange("p t (c i) -> p c t i", i=4),
+            )
+
+        def quant_page(b, half):
+            codes = keep.tile([P, HALF], U32, name="page_codes%d_%d" % (b, half), align_bytes=64)
+            scales = keep.tile([P, HALF], U8, name="page_scales%d_%d" % (b, half), align_bytes=64)
+            nc.vector.quantize_mx(
+                out=codes[:].bitcast(FP8X4), scales=scales[:], in_=page_bf[b, half].rearrange("p c t -> p (c t)")
+            )
+            page_codes[b, half], page_scales[b, half] = codes, scales
+
+        cast_w1(0, 0, 0)
+        cast_w1(1, 0, 84)
+        quant_w1(0, 0)
+        quant_w1(1, 0)
+
+        def weave_last_plane(t, half):
+            cols = slice(HALF * half, HALF * (half + 1))
+            nc.scalar.copy(out=page_bf[last, half][:, :, t], in_=page_t[PACK * last + t][:, cols])
+
+        due_t = []
+        for n in range(TILES):
+            b, t = divmod(n, PACK)
+            if n >= 2:
+                make_x(n - 2)
+            h, weight = make_h(n)
+            if n >= 1:
+                gather(n - 1)
+            if n == TILES - 1:
+                quant_x(last - 1)
+            scatter(n, h, weight)
+            if n == 0:
+                front(1)
+                nc.scalar.mul(out=wg_rest[:, 0, :], in_=wg_rest[:, 0, :], mul=2.0)
+            if n + 1 < TILES:
+                turn_back(n + 1)
+            if n + AHEAD < TILES:
+                front(n + AHEAD)
+            if n in (0, 1):
+                nc.scalar.mul(out=wg_rest[:, n + 1, :], in_=wg_rest[:, n + 1, :], mul=2.0)
+            if n == 2:
+                nc.scalar.mul(out=wg_first2[:], in_=wg_first[:], mul=2.0)
+            if n + 4 < TILES:
+                load_lim(n + 4)
+            if n + PAGE_AHEAD < TILES:
+                load_page(n + PAGE_AHEAD)
+            if b < last and t < A_PASSES:
+                cast_w1(t, b + 1, 0)
+                quant_w1(t, b + 1)
+            if n in (2, 3):
+                load_w1(2, n - 2)
+            if n in (6, 7):
+                d = ring.tile([P, M_TILES // 2, NP], F32, name="due", tag="w1_raw")
+                rows = due[HALF * (n - 6) : HALF * (n - 5), :]
+                nc.sync.dma_start(out=d[:], in_=rows.rearrange("(i p) j -> p i j", p=P))
+                due_t.append(d)
+            if b > 0 and t in (1, 2):
+                weave_page(b - 1, t - 1, PACK)
+                quant_page(b - 1, t - 1)
+            if b > 0 and t == 2:
+                weave_x(b - 1)
+                if b < last:
+                    quant_x(b - 1)
+
+        make_x(TILES - 2)
+        gather(TILES - 1)
+        for half in range(2):
+            weave_page(last, half, PACK - 1)
+        for half in range(2):
+            weave_last_plane(PACK - 1, half)
+        make_x(TILES - 1)
+        quant_page(last, 0)
+        quant_x(last)
+        quant_page(last, 1)
+
+        scores = [bank((m + RING_BANKS) % M_TILES, [P, NP]) for m in range(M_TILES)]
+        for b in range(R_PASSES):
+            for m in range(M_TILES):
+                half, c = divmod(m, M_TILES // 2)
+                cols = slice(P * c, P * (c + 1))
+                nc.tensor.matmul_mx(
+                    out=scores[m][:],
+                    lhsT=page_codes[b, half][:, cols].bitcast(FP8X4),
+                    lhsT_scale=page_scales[b, half][:, cols],
+                    rhs=x_codes[b][:].bitcast(FP8X4),
+                    rhs_scale=x_scales[b][:],
+                    start=(b == 0),
+                    stop=(b == last),
+                )
+        for m in range(M_TILES):
+            half, c = divmod(m, M_TILES // 2)
+            y = ring.tile([P, NP], F32, name="y", tag="lim", bufs=4)
+            nc.vector.tensor_tensor(out=y[:], in0=scores[m][:], in1=due_t[half][:, c, :], op=ALU.subtract)
+            res = ring.tile([P, NP], F32, name="res", tag="page", bufs=6)
+            nc.scalar.activation(out=res[:], in_=y[:], func=ACT.Silu)
+            nc.sync.dma_start(out=out[P * m : P * (m + 1), :], in_=res[:])

@@ -26,8 +26,10 @@ TILES = R_PASSES * PACK
 M_TILES = T2 // P
 QUAD = 32
 AHEAD = 2
-PAGE_AHEAD = 3
+PAGE_AHEAD = 4
 RING_BANKS = 4
+VECTOR_M = 36
+W1_BF = [P, PACK, P, PACK]
 
 
 def tile_list_vanilla_page_scores_kernel(
@@ -43,28 +45,22 @@ def tile_list_vanilla_page_scores_kernel(
         def bank(i, shape):
             return psum.tile(shape, F32, name="bank%d" % i, tag="bank%d" % i)
 
+        def slot(n, shape, dtype, name):
+            return keep.tile(shape, dtype, name=name, tag="slot%d" % n, align_bytes=64)
+
+        def turn(n, shape, dtype, name):
+            return keep.tile(shape, dtype, name=name, tag="turn%d" % (n % 2), align_bytes=64)
+
         idx1 = lists.tile([P, S // 16], U16)
         idx2 = lists.tile([P, S // 16], U16)
         idx3 = lists.tile([P, NP // 16], U16)
         nc.sync.dma_start(idx1[:], offs)
-        nc.sync.dma_start(idx2[:], offs2)
-        nc.sync.dma_start(idx3[:], offs3)
-        row_consts = []
-        for name, v in (("cen", cen), ("cap", cap), ("vec", vec)):
-            cols = keep.tile([P, R_PASSES, PACK], F32, name=name)
-            nc.sync.dma_start(out=cols[:], in_=v.rearrange("(b p t) -> p b t", p=P, t=PACK))
-            row_consts.append(cols)
-        cen_c, cap_c, vec_c = row_consts
         w4_raw = keep.tile([P, A_PASSES, 2 * H], U8, align_bytes=64)
         nc.sync.dma_start(out=w4_raw[:].bitcast(I32), in_=w4_words.rearrange("a p n -> p a n").bitcast(I32))
         tab_sc = keep.tile([P, A_PASSES, T], U8, align_bytes=64)
         w4_sc = keep.tile([P, A_PASSES, H], U8, align_bytes=64)
-        nc.vector.memset(w4_sc[:].rearrange("p a n -> p (a n)").bitcast(I32), 0)
+        nc.gpsimd.memset(w4_sc[:].rearrange("p a n -> p (a n)").bitcast(I32), 0)
         nc.vector.memset(tab_sc[:].rearrange("p a n -> p (a n)").bitcast(I32), 0)
-        ident = keep.tile([P, P], F32)
-        make_identity(nc, ident[:])
-        warm = keep.tile([P, 1], F32)
-        nc.scalar.activation(out=warm[:], in_=ident[:, 0:1], func=ACT.Silu)
 
         tab = []
 
@@ -74,17 +70,19 @@ def tile_list_vanilla_page_scores_kernel(
             tab.append(words)
 
         def load_scale_rows(plane, rows, q):
-            nc.sync.dma_start(
-                out=plane[QUAD * q : QUAD * q + 4, :, :].bitcast(I32),
-                in_=rows[:, 4 * q : 4 * q + 4, :].rearrange("a q n -> q a n").bitcast(I32),
+            nc.gpsimd.dma_start(
+                out=plane[q:P:QUAD, :, :].bitcast(I32),
+                in_=rows[:, q:16:4, :].rearrange("a q n -> q a n").bitcast(I32),
             )
 
         w1_raw = {}
 
-        def load_w1(b, a):
-            raw = ring.tile([P, PACK, KP], F32, name="w1_raw")
-            rows = w1[KP * a : KP * (a + 1), KP * b : KP * (b + 1)]
-            nc.sync.dma_start(out=raw[:], in_=rows.rearrange("(p j) c -> p j c", j=PACK))
+        def load_w1(b, a, pieces=1):
+            width = KP // pieces
+            raw = ring.tile([P, pieces, PACK, width], F32, name="w1_raw", bufs=3)
+            for k in range(pieces):
+                rows = w1[KP * a : KP * (a + 1), KP * b + width * k : KP * b + width * (k + 1)]
+                nc.sync.dma_start(out=raw[:, k], in_=rows.rearrange("(p j) c -> p j c", j=PACK))
             w1_raw[a, b] = raw
 
         lim_t, page_t = {}, {}
@@ -94,49 +92,67 @@ def tile_list_vanilla_page_scores_kernel(
             return x[KP * b : KP * (b + 1), :].rearrange("(p t) c -> p t c", t=PACK)[:, t, :]
 
         def load_lim(n):
-            lim_t[n] = ring.tile([P, S], F32, name="lim", bufs=4)
-            nc.sync.dma_start(out=lim_t[n][:], in_=rows_of(lim, n))
+            b, t = divmod(n, PACK)
+            pair = ring.tile([P, 2, S], F32, name="lim", bufs=3)
+            rows = lim[KP * b : KP * (b + 1), :].rearrange("(p t) c -> p t c", t=PACK)
+            nc.sync.dma_start(out=pair[:], in_=rows[:, t : t + 2, :])
+            lim_t[n], lim_t[n + 1] = pair[:, 0, :], pair[:, 1, :]
 
         def load_page(n):
             page_t[n] = ring.tile([P, T2], F32, name="page", bufs=6)
             nc.sync.dma_start(out=page_t[n][:], in_=rows_of(page0, n))
 
-        load_tab(0)
-        for q in (0, 2, 1, 3):
-            load_scale_rows(w4_sc, w4_scales, q)
-        for q in (0, 2):
-            load_scale_rows(tab_sc, tab_scales, q)
-        load_tab(1)
-        load_w1(0, 0)
-        for q in (1, 3):
-            load_scale_rows(tab_sc, tab_scales, q)
-        load_w1(0, 1)
-        load_lim(0)
         wgs_v = wgs.rearrange("(p t) j -> p t j", t=PACK)
-        wg_first = keep.tile([P, S], F32)
-        for q in range(P // QUAD):
-            nc.sync.dma_start(out=wg_first[QUAD * q : QUAD * (q + 1), :], in_=wgs_v[:, 0, :])
+        weight_t = {}
+
+        def load_wgs(t0, t1, queue):
+            planes = keep.tile([P, t1 - t0, S], F32, name="wgs%d" % t0)
+            for q in range(P // QUAD):
+                queue.dma_start(out=planes[QUAD * q : QUAD * (q + 1), :, :], in_=wgs_v[:, t0:t1, :])
+            for t in range(t0, t1):
+                weight_t[t] = planes[:, t - t0, :]
+
+        load_wgs(0, 2, nc.scalar)
+        row_consts = []
+        for name, v in (("cen", cen), ("cap", cap), ("vec", vec)):
+            cols = keep.tile([P, R_PASSES, PACK], F32, name=name)
+            nc.scalar.dma_start(out=cols[:], in_=v.rearrange("(b p t) -> p b t", p=P, t=PACK))
+            row_consts.append(cols)
+        cen_c, cap_c, vec_c = row_consts
+        warm = keep.tile([P, 1], F32)
+        nc.scalar.activation(out=warm[:], in_=weight_t[0][:, 0:1], func=ACT.Silu)
+        for q in range(4):
+            load_scale_rows(w4_sc, w4_scales, q)
+        for q in range(4):
+            load_scale_rows(tab_sc, tab_scales, q)
+        load_tab(0)
+        load_w1(0, 0)
+        load_tab(1)
+        load_w1(0, 1, 2)
+        load_lim(0)
+        nc.sync.dma_start(idx2[:], offs2)
         load_page(0)
-        load_lim(1)
+        nc.sync.dma_start(idx3[:], offs3)
         load_w1(1, 0)
-        wg_rest = keep.tile([P, PACK - 1, S], F32)
-        for q in range(P // QUAD):
-            nc.sync.dma_start(out=wg_rest[QUAD * q : QUAD * (q + 1), :, :], in_=wgs_v[:, 1:PACK, :])
         load_page(1)
         load_w1(1, 1)
         load_lim(2)
+        load_wgs(2, 3, nc.sync)
         load_page(2)
-        load_lim(3)
+        load_wgs(3, 4, nc.sync)
+        load_page(3)
 
+        ident = keep.tile([P, P], F32)
+        make_identity(nc, ident[:])
         w4_dealt = keep.tile([P, A_PASSES * R_PASSES, PACK, 2 * P], U8, align_bytes=64)
         nc.vector.tensor_copy(
-            out=w4_dealt[:].bitcast(U16).rearrange("p g t (o i) -> p g o t i", i=8),
-            in_=w4_raw[:].rearrange("p a n -> p (a n)").bitcast(U16).rearrange("p (g o i t) -> p g o t i", o=16, i=8, t=PACK),
+            out=w4_dealt[:].bitcast(U16),
+            in_=w4_raw[:].rearrange("p a n -> p (a n)").bitcast(U16).rearrange("p (g m t) -> p g t m", m=P, t=PACK),
         )
         w4_sc_dealt = keep.tile([P, A_PASSES * R_PASSES, PACK, P], U8, align_bytes=64)
         nc.vector.tensor_copy(
-            out=w4_sc_dealt[:].rearrange("p g t (o i) -> p g o t i", i=16),
-            in_=w4_sc[:].rearrange("p a n -> p (a n)").rearrange("p (g o i t) -> p g o t i", o=8, i=16, t=PACK),
+            out=w4_sc_dealt[:],
+            in_=w4_sc[:].rearrange("p a n -> p (a n)").rearrange("p (g m t) -> p g t m", m=P, t=PACK),
         )
 
         v_words, v_scales = [], []
@@ -151,26 +167,32 @@ def tile_list_vanilla_page_scores_kernel(
 
         w1_bf, w1_codes, w1_scales = {}, {}, {}
 
-        def cast_w1(a, b, vector_m):
-            grouped = ring.tile([P, PACK, P, PACK], BF16, name="w1_bf", align_bytes=64)
-            dst = grouped[:].rearrange("p t m j -> p m j t")
-            src = w1_raw[a, b][:].rearrange("p j (m t) -> p m j t", t=PACK)
-            if vector_m > 0:
-                nc.vector.tensor_copy(out=dst[:, 0:vector_m], in_=src[:, 0:vector_m])
-            nc.scalar.copy(out=dst[:, vector_m:P], in_=src[:, vector_m:P])
+        def cast_w1(a, b, grouped):
             w1_bf[a, b] = grouped
+            dst = grouped[:].rearrange("p t m j -> p m j t")
+            if (a, b) != (A_PASSES - 1, 0):
+                nc.scalar.copy(out=dst, in_=w1_raw[a, b][:, 0].rearrange("p j (m t) -> p m j t", t=PACK))
+                return
+            half = P // 2
+            early, late = [w1_raw[a, b][:, k].rearrange("p j (m t) -> p m j t", t=PACK) for k in range(2)]
+            nc.scalar.copy(out=dst[:, 0:half], in_=early)
+            nc.vector.tensor_copy(out=dst[:, half : half + VECTOR_M], in_=late[:, 0:VECTOR_M])
+            nc.scalar.copy(out=dst[:, half + VECTOR_M : P], in_=late[:, VECTOR_M:half])
 
-        def quant_w1(a, b):
+        def quant_w1(a, b, spans):
             codes = ring.tile([P, KP], U32, name="w1_codes", bufs=4, align_bytes=64)
             scales = ring.tile([P, KP], U8, name="w1_scales", bufs=4, align_bytes=64)
-            nc.vector.quantize_mx(
-                out=codes[:].bitcast(FP8X4), scales=scales[:], in_=w1_bf[a, b][:].rearrange("p t m j -> p (t m j)")
-            )
+            for t0, t1 in spans:
+                nc.vector.quantize_mx(
+                    out=codes[:, P * t0 : P * t1].bitcast(FP8X4),
+                    scales=scales[:, P * t0 : P * t1],
+                    in_=w1_bf[a, b][:, t0:t1].rearrange("p t m j -> p (t m j)"),
+                )
             w1_codes[a, b], w1_scales[a, b] = codes, scales
 
         def first_product(n):
             b, t = divmod(n, PACK)
-            acc = bank((n + 2) % RING_BANKS, [P, S])
+            acc = bank((n + 2) % RING_BANKS if n > 0 else 0, [P, S])
             cols = slice(P * t, P * (t + 1))
             for a in range(A_PASSES):
                 g = R_PASSES * a + b
@@ -201,10 +223,7 @@ def tile_list_vanilla_page_scores_kernel(
 
         def front(n):
             acc = first_product(n)
-            if n < TILES - 1:
-                a_sb[n] = ring.tile([P, S], F32, name="a_sb")
-            else:
-                a_sb[n] = ring.tile([P, S], F32, name="a_sb_last", tag="late", bufs=1, align_bytes=64)
+            a_sb[n] = slot(n, [P, S], F32, "a_sb")
             nc.scalar.copy(out=a_sb[n][:], in_=acc[:])
             turned = bank(RING_BANKS + n % RING_BANKS, [P, S // P, P])
             for c in range(S // P):
@@ -221,18 +240,16 @@ def tile_list_vanilla_page_scores_kernel(
             for c in range(S // P):
                 nc.tensor.transpose(half_sum[n][:, c, :], turned_sb[:, c, :], ident[:])
 
-        wg_first2 = keep.tile([P, S], F32)
-
         def make_h(n):
-            h = ring.tile([P, S], F32, name="h")
+            h = keep.tile([P, S], F32, name="h", tag="h")
             if n == 0:
                 acc = first_product(0)
-                relu2 = ring.tile([P, S], F32, name="a_sb")
-                nc.scalar.activation(out=relu2[:], in_=acc[:], func=ACT.Relu, scale=2.0)
                 total = ring.tile([P, S], F32, name="total", tag="step", bufs=1, align_bytes=64)
-                nc.vector.tensor_tensor(out=total[:], in0=acc[:], in1=lim_t[0][:], op=ALU.add)
-                nc.vector.tensor_tensor(out=h[:], in0=total[:], in1=relu2[:], op=ALU.min)
-                return h, wg_first[:]
+                nc.vector.scalar_tensor_tensor(
+                    out=total[:], in0=acc[:], scalar=0.5, in1=half_lim[:], op0=ALU.mult, op1=ALU.add
+                )
+                nc.vector.scalar_tensor_tensor(out=h[:], in0=acc[:], scalar=0.0, in1=total[:], op0=ALU.max, op1=ALU.min)
+                return h
             nc.vector.scalar_tensor_tensor(
                 out=h[:],
                 in0=a_sb[n][:],
@@ -241,8 +258,7 @@ def tile_list_vanilla_page_scores_kernel(
                 op0=ALU.max,
                 op1=ALU.min,
             )
-            t = n % PACK
-            return h, (wg_first2[:] if t == 0 else wg_rest[:, t - 1, :])
+            return h
 
         staged, page_bf, x_planes, x_bf, picked = {}, {}, {}, {}, {}
         last = R_PASSES - 1
@@ -251,20 +267,22 @@ def tile_list_vanilla_page_scores_kernel(
             picked[n] = ring.tile([P, NP], F32, name="picked", bufs=1)
             nc.vector.tensor_copy(out=picked[n][:], in_=page_t[n][:].indirect(idx3[:]))
 
-        def scatter(n, h, weight):
+        def scatter(n, h):
             b, t = divmod(n, PACK)
-            nc.vector.tensor_tensor(out=page_t[n][:].indirect(idx2[:]), in0=h[:], in1=weight, op=ALU.mult)
-            if n < TILES - 1:
-                if t == 0:
-                    staged[b] = ring.tile([P, PACK, T2], F32, name="staged", align_bytes=64)
-                nc.sync.dma_start(out=staged[b][:, t, :], in_=page_t[n][:])
+            nc.vector.tensor_tensor(out=page_t[n][:].indirect(idx2[:]), in0=h[:], in1=weight_t[t], op=ALU.mult)
+
+        def stage(n):
+            b, t = divmod(n, PACK)
+            if t == 0:
+                staged[b] = ring.tile([P, PACK, T2], F32, name="staged", align_bytes=64)
+            nc.sync.dma_start(out=staged[b][:, t, :], in_=page_t[n][:])
 
         def make_x(n):
             b, t = divmod(n, PACK)
             if n < TILES - 2:
                 u = ring.tile([P, NP], F32, name="u", tag="step", bufs=1, align_bytes=64)
             else:
-                u = ring.tile([P, NP], F32, name="u_last", tag="a_sb")
+                u = ring.tile([P, NP], F32, name="u_last", tag="lim", bufs=3)
             nc.vector.tensor_scalar(
                 out=u[:],
                 in0=picked[n][:],
@@ -286,8 +304,8 @@ def tile_list_vanilla_page_scores_kernel(
                 else:
                     nc.vector.tensor_scalar(out=x_bf[b][:, :, t], in0=u[:], scalar1=factor, scalar2=None, op0=ALU.mult)
 
-        def weave_x(b):
-            x_bf[b] = ring.tile([P, NP, PACK], BF16, name="x_bf", align_bytes=64)
+        def weave_x(b, n):
+            x_bf[b] = slot(n, [P, NP, PACK], BF16, "x_bf")
             nc.scalar.copy(
                 out=x_bf[b][:].rearrange("p (c i) t -> p c t i", i=4),
                 in_=x_planes[b][:].rearrange("p t (c i) -> p c t i", i=4),
@@ -295,11 +313,8 @@ def tile_list_vanilla_page_scores_kernel(
 
         x_codes, x_scales, page_codes, page_scales = {}, {}, {}, {}
 
-        def quant_x(b):
-            if b == last - 1:
-                x_codes[b] = ring.tile([P, NP], U32, name="x_codes_late", tag="late", bufs=1, align_bytes=64)
-            else:
-                x_codes[b] = keep.tile([P, NP], U32, name="x_codes%d" % b, align_bytes=64)
+        def quant_x(b, n):
+            x_codes[b] = slot(n, [P, NP], U32, "x_codes")
             x_scales[b] = keep.tile([P, NP], U8, name="x_scales%d" % b, align_bytes=64)
             nc.vector.quantize_mx(
                 out=x_codes[b][:].bitcast(FP8X4), scales=x_scales[b][:], in_=x_bf[b][:].rearrange("p c t -> p (c t)")
@@ -307,9 +322,9 @@ def tile_list_vanilla_page_scores_kernel(
 
         HALF = T2 // 2
 
-        def weave_page(b, half, planes):
+        def weave_page(b, half, planes, n):
             if b < last:
-                piece = ring.tile([P, HALF, PACK], BF16, name="page_bf", align_bytes=64)
+                piece = turn(n, [P, HALF, PACK], BF16, "page_bf")
                 page_bf[b, half] = piece[:]
             elif half == 0:
                 whole = ring.tile([P, 2, HALF, PACK], BF16, name="page_last", tag="step", bufs=1, align_bytes=64)
@@ -328,68 +343,75 @@ def tile_list_vanilla_page_scores_kernel(
             )
             page_codes[b, half], page_scales[b, half] = codes, scales
 
-        cast_w1(0, 0, 0)
-        cast_w1(1, 0, 84)
-        quant_w1(0, 0)
-        quant_w1(1, 0)
+        cast_w1(0, 0, turn(0, W1_BF, BF16, "w1_bf"))
+        quant_w1(0, 0, [(0, PACK)])
+        cast_w1(1, 0, turn(1, W1_BF, BF16, "w1_bf"))
+        quant_w1(1, 0, [(0, 1), (1, 2), (2, PACK)])
+        half_lim = keep.tile([P, S], F32)
+        nc.scalar.mul(out=half_lim[:], in_=lim_t[0], mul=0.5)
+        nc.scalar.mul(out=weight_t[0], in_=weight_t[0], mul=2.0)
 
         def weave_last_plane(t, half):
             cols = slice(HALF * half, HALF * (half + 1))
             nc.scalar.copy(out=page_bf[last, half][:, :, t], in_=page_t[PACK * last + t][:, cols])
+
+        w1_steps = {0: (0, 1), 1: (1, 1), 4: (0, 2), 5: (1, 2)}
+        page_steps = {6: (0, 0), 7: (0, 1), 9: (1, 0), 10: (1, 1)}
+        x_steps = {8: 0, 9: 1}
 
         due_t = []
         for n in range(TILES):
             b, t = divmod(n, PACK)
             if n >= 2:
                 make_x(n - 2)
-            h, weight = make_h(n)
+            h = make_h(n)
             if n >= 1:
                 gather(n - 1)
             if n == TILES - 1:
-                quant_x(last - 1)
-            scatter(n, h, weight)
+                quant_x(0, TILES - 1)
+                quant_x(1, 1)
+            scatter(n, h)
             if n == 0:
                 front(1)
-                nc.scalar.mul(out=wg_rest[:, 0, :], in_=wg_rest[:, 0, :], mul=2.0)
+            if n + 1 < PACK:
+                nc.scalar.mul(out=weight_t[n + 1], in_=weight_t[n + 1], mul=2.0)
             if n + 1 < TILES:
                 turn_back(n + 1)
             if n + AHEAD < TILES:
                 front(n + AHEAD)
-            if n in (0, 1):
-                nc.scalar.mul(out=wg_rest[:, n + 1, :], in_=wg_rest[:, n + 1, :], mul=2.0)
-            if n == 2:
-                nc.scalar.mul(out=wg_first2[:], in_=wg_first[:], mul=2.0)
-            if n + 4 < TILES:
+            if n % 2 == 0 and n + 4 < TILES:
                 load_lim(n + 4)
             if n + PAGE_AHEAD < TILES:
                 load_page(n + PAGE_AHEAD)
-            if b < last and t < A_PASSES:
-                cast_w1(t, b + 1, 0)
-                quant_w1(t, b + 1)
-            if n in (2, 3):
-                load_w1(2, n - 2)
+            if n in (0, 1):
+                load_w1(2, n)
+            if n < TILES - 1:
+                stage(n)
+            if n in w1_steps:
+                a, group = w1_steps[n]
+                cast_w1(a, group, turn(n, W1_BF, BF16, "w1_bf") if n > 0 else slot(0, W1_BF, BF16, "w1_bf"))
+                quant_w1(a, group, [(0, PACK)])
+            if n in page_steps:
+                group, half = page_steps[n]
+                weave_page(group, half, PACK, n)
+                quant_page(group, half)
+            if n in x_steps:
+                weave_x(x_steps[n], n)
             if n in (6, 7):
-                d = ring.tile([P, M_TILES // 2, NP], F32, name="due", tag="w1_raw")
+                d = ring.tile([P, M_TILES // 2, NP], F32, name="due", tag="w1_raw", bufs=3)
                 rows = due[HALF * (n - 6) : HALF * (n - 5), :]
                 nc.sync.dma_start(out=d[:], in_=rows.rearrange("(i p) j -> p i j", p=P))
                 due_t.append(d)
-            if b > 0 and t in (1, 2):
-                weave_page(b - 1, t - 1, PACK)
-                quant_page(b - 1, t - 1)
-            if b > 0 and t == 2:
-                weave_x(b - 1)
-                if b < last:
-                    quant_x(b - 1)
 
         make_x(TILES - 2)
         gather(TILES - 1)
         for half in range(2):
-            weave_page(last, half, PACK - 1)
+            weave_page(last, half, PACK - 1, TILES)
         for half in range(2):
             weave_last_plane(PACK - 1, half)
         make_x(TILES - 1)
         quant_page(last, 0)
-        quant_x(last)
+        quant_x(last, 2)
         quant_page(last, 1)
 
         scores = [bank((m + RING_BANKS) % M_TILES, [P, NP]) for m in range(M_TILES)]
@@ -408,7 +430,7 @@ def tile_list_vanilla_page_scores_kernel(
                 )
         for m in range(M_TILES):
             half, c = divmod(m, M_TILES // 2)
-            y = ring.tile([P, NP], F32, name="y", tag="lim", bufs=4)
+            y = ring.tile([P, NP], F32, name="y", tag="lim", bufs=3)
             nc.vector.tensor_tensor(out=y[:], in0=scores[m][:], in1=due_t[half][:, c, :], op=ALU.subtract)
             res = ring.tile([P, NP], F32, name="res", tag="page", bufs=6)
             nc.scalar.activation(out=res[:], in_=y[:], func=ACT.Silu)

@@ -55,10 +55,15 @@ def tile_list_vanilla_page_scores_kernel(
         idx2 = lists.tile([P, S // 16], U16)
         idx3 = lists.tile([P, NP // 16], U16)
         nc.sync.dma_start(idx1[:], offs)
-        w4_raw = keep.tile([P, A_PASSES, 2 * H], U8, align_bytes=64)
-        nc.sync.dma_start(out=w4_raw[:].bitcast(I32), in_=w4_words.rearrange("a p n -> p a n").bitcast(I32))
+        w4_raw = [keep.tile([P, 2 * H], U8, name="w4_raw%d" % a, align_bytes=64) for a in range(A_PASSES)]
+        for a in range(A_PASSES):
+            nc.sync.dma_start(out=w4_raw[a][:].bitcast(I32), in_=w4_words[a].bitcast(I32))
         tab_sc = keep.tile([P, A_PASSES, T], U8, align_bytes=64)
         w4_sc = keep.tile([P, A_PASSES, H], U8, align_bytes=64)
+        warm_in = keep.tile([P, 1], F32)
+        warm_out = keep.tile([P, 1], F32)
+        nc.vector.memset(warm_in[:], 0.0)
+        nc.scalar.activation(out=warm_out[:], in_=warm_in[:], func=ACT.Silu)
         nc.gpsimd.memset(w4_sc[:].rearrange("p a n -> p (a n)").bitcast(I32), 0)
         nc.vector.memset(tab_sc[:].rearrange("p a n -> p (a n)").bitcast(I32), 0)
 
@@ -119,12 +124,10 @@ def tile_list_vanilla_page_scores_kernel(
             nc.scalar.dma_start(out=cols[:], in_=v.rearrange("(b p t) -> p b t", p=P, t=PACK))
             row_consts.append(cols)
         cen_c, cap_c, vec_c = row_consts
-        warm = keep.tile([P, 1], F32)
-        nc.scalar.activation(out=warm[:], in_=weight_t[0][:, 0:1], func=ACT.Silu)
-        for q in range(4):
-            load_scale_rows(w4_sc, w4_scales, q)
         for q in range(4):
             load_scale_rows(tab_sc, tab_scales, q)
+        for q in range(4):
+            load_scale_rows(w4_sc, w4_scales, q)
         load_tab(0)
         load_w1(0, 0)
         load_tab(1)
@@ -145,10 +148,11 @@ def tile_list_vanilla_page_scores_kernel(
         ident = keep.tile([P, P], F32)
         make_identity(nc, ident[:])
         w4_dealt = keep.tile([P, A_PASSES * R_PASSES, PACK, 2 * P], U8, align_bytes=64)
-        nc.vector.tensor_copy(
-            out=w4_dealt[:].bitcast(U16),
-            in_=w4_raw[:].rearrange("p a n -> p (a n)").bitcast(U16).rearrange("p (g m t) -> p g t m", m=P, t=PACK),
-        )
+        for a in range(A_PASSES):
+            nc.vector.tensor_copy(
+                out=w4_dealt[:, R_PASSES * a : R_PASSES * (a + 1)].bitcast(U16),
+                in_=w4_raw[a][:].bitcast(U16).rearrange("p (b m t) -> p b t m", m=P, t=PACK),
+            )
         w4_sc_dealt = keep.tile([P, A_PASSES * R_PASSES, PACK, P], U8, align_bytes=64)
         nc.vector.tensor_copy(
             out=w4_sc_dealt[:],
@@ -169,12 +173,12 @@ def tile_list_vanilla_page_scores_kernel(
 
         def cast_w1(a, b, grouped):
             w1_bf[a, b] = grouped
-            dst = grouped[:].rearrange("p t m j -> p m j t")
+            dst = grouped[:].rearrange("p t m j -> p m t j")
             if (a, b) != (A_PASSES - 1, 0):
-                nc.scalar.copy(out=dst, in_=w1_raw[a, b][:, 0].rearrange("p j (m t) -> p m j t", t=PACK))
+                nc.scalar.copy(out=dst, in_=w1_raw[a, b][:, 0].rearrange("p j (m t) -> p m t j", t=PACK))
                 return
             half = P // 2
-            early, late = [w1_raw[a, b][:, k].rearrange("p j (m t) -> p m j t", t=PACK) for k in range(2)]
+            early, late = [w1_raw[a, b][:, k].rearrange("p j (m t) -> p m t j", t=PACK) for k in range(2)]
             nc.scalar.copy(out=dst[:, 0:half], in_=early)
             nc.vector.tensor_copy(out=dst[:, half : half + VECTOR_M], in_=late[:, 0:VECTOR_M])
             nc.scalar.copy(out=dst[:, half + VECTOR_M : P], in_=late[:, VECTOR_M:half])
@@ -307,8 +311,8 @@ def tile_list_vanilla_page_scores_kernel(
         def weave_x(b, n):
             x_bf[b] = slot(n, [P, NP, PACK], BF16, "x_bf")
             nc.scalar.copy(
-                out=x_bf[b][:].rearrange("p (c i) t -> p c t i", i=4),
-                in_=x_planes[b][:].rearrange("p t (c i) -> p c t i", i=4),
+                out=x_bf[b][:],
+                in_=x_planes[b][:].rearrange("p t c -> p c t"),
             )
 
         x_codes, x_scales, page_codes, page_scales = {}, {}, {}, {}
@@ -331,8 +335,8 @@ def tile_list_vanilla_page_scores_kernel(
                 page_bf[b, 0], page_bf[b, 1] = whole[:, 0], whole[:, 1]
             src = staged[b][:, 0:planes, HALF * half : HALF * (half + 1)]
             nc.scalar.copy(
-                out=page_bf[b, half].rearrange("p (c i) t -> p c t i", i=4)[:, :, 0:planes, :],
-                in_=src.rearrange("p t (c i) -> p c t i", i=4),
+                out=page_bf[b, half][:, :, 0:planes],
+                in_=src.rearrange("p t c -> p c t"),
             )
 
         def quant_page(b, half):

@@ -60,10 +60,6 @@ def tile_list_vanilla_page_scores_kernel(
             nc.sync.dma_start(out=w4_raw[a][:].bitcast(I32), in_=w4_words[a].bitcast(I32))
         tab_sc = keep.tile([P, A_PASSES, T], U8, align_bytes=64)
         w4_sc = keep.tile([P, A_PASSES, H], U8, align_bytes=64)
-        warm_in = keep.tile([P, 1], F32)
-        warm_out = keep.tile([P, 1], F32)
-        nc.vector.memset(warm_in[:], 0.0)
-        nc.scalar.activation(out=warm_out[:], in_=warm_in[:], func=ACT.Silu)
         nc.gpsimd.memset(w4_sc[:].rearrange("p a n -> p (a n)").bitcast(I32), 0)
         nc.vector.memset(tab_sc[:].rearrange("p a n -> p (a n)").bitcast(I32), 0)
 
@@ -98,9 +94,9 @@ def tile_list_vanilla_page_scores_kernel(
 
         def load_lim(n):
             b, t = divmod(n, PACK)
-            pair = ring.tile([P, 2, S], F32, name="lim", bufs=3)
+            pair = ring.tile([P, 2, S], F32, name="lim")
             rows = lim[KP * b : KP * (b + 1), :].rearrange("(p t) c -> p t c", t=PACK)
-            nc.sync.dma_start(out=pair[:], in_=rows[:, t : t + 2, :])
+            (nc.sync if n < PACK else nc.scalar).dma_start(out=pair[:], in_=rows[:, t : t + 2, :])
             lim_t[n], lim_t[n + 1] = pair[:, 0, :], pair[:, 1, :]
 
         def load_page(n):
@@ -124,10 +120,12 @@ def tile_list_vanilla_page_scores_kernel(
             nc.scalar.dma_start(out=cols[:], in_=v.rearrange("(b p t) -> p b t", p=P, t=PACK))
             row_consts.append(cols)
         cen_c, cap_c, vec_c = row_consts
-        for q in range(4):
-            load_scale_rows(tab_sc, tab_scales, q)
+        warm = keep.tile([P, 1], F32)
+        nc.scalar.activation(out=warm[:], in_=weight_t[0][:, 0:1], func=ACT.Silu)
         for q in range(4):
             load_scale_rows(w4_sc, w4_scales, q)
+        for q in range(4):
+            load_scale_rows(tab_sc, tab_scales, q)
         load_tab(0)
         load_w1(0, 0)
         load_tab(1)
@@ -136,10 +134,10 @@ def tile_list_vanilla_page_scores_kernel(
         nc.sync.dma_start(idx2[:], offs2)
         load_page(0)
         nc.sync.dma_start(idx3[:], offs3)
+        load_lim(2)
         load_w1(1, 0)
         load_page(1)
         load_w1(1, 1)
-        load_lim(2)
         load_wgs(2, 3, nc.sync)
         load_page(2)
         load_wgs(3, 4, nc.sync)
@@ -150,8 +148,8 @@ def tile_list_vanilla_page_scores_kernel(
         w4_dealt = keep.tile([P, A_PASSES * R_PASSES, PACK, 2 * P], U8, align_bytes=64)
         for a in range(A_PASSES):
             nc.vector.tensor_copy(
-                out=w4_dealt[:, R_PASSES * a : R_PASSES * (a + 1)].bitcast(U16),
-                in_=w4_raw[a][:].bitcast(U16).rearrange("p (b m t) -> p b t m", m=P, t=PACK),
+                out=w4_dealt[:, R_PASSES * a : R_PASSES * (a + 1)].bitcast(U16).rearrange("p b t m -> p t b m"),
+                in_=w4_raw[a][:].bitcast(U16).rearrange("p (b m t) -> p t b m", m=P, t=PACK),
             )
         w4_sc_dealt = keep.tile([P, A_PASSES * R_PASSES, PACK, P], U8, align_bytes=64)
         nc.vector.tensor_copy(
@@ -173,12 +171,12 @@ def tile_list_vanilla_page_scores_kernel(
 
         def cast_w1(a, b, grouped):
             w1_bf[a, b] = grouped
-            dst = grouped[:].rearrange("p t m j -> p m t j")
+            dst = grouped[:].rearrange("p t m j -> p m j t")
             if (a, b) != (A_PASSES - 1, 0):
-                nc.scalar.copy(out=dst, in_=w1_raw[a, b][:, 0].rearrange("p j (m t) -> p m t j", t=PACK))
+                nc.scalar.copy(out=dst, in_=w1_raw[a, b][:, 0].rearrange("p j (m t) -> p m j t", t=PACK))
                 return
             half = P // 2
-            early, late = [w1_raw[a, b][:, k].rearrange("p j (m t) -> p m t j", t=PACK) for k in range(2)]
+            early, late = [w1_raw[a, b][:, k].rearrange("p j (m t) -> p m j t", t=PACK) for k in range(2)]
             nc.scalar.copy(out=dst[:, 0:half], in_=early)
             nc.vector.tensor_copy(out=dst[:, half : half + VECTOR_M], in_=late[:, 0:VECTOR_M])
             nc.scalar.copy(out=dst[:, half + VECTOR_M : P], in_=late[:, VECTOR_M:half])
@@ -230,10 +228,17 @@ def tile_list_vanilla_page_scores_kernel(
             a_sb[n] = slot(n, [P, S], F32, "a_sb")
             nc.scalar.copy(out=a_sb[n][:], in_=acc[:])
             turned = bank(RING_BANKS + n % RING_BANKS, [P, S // P, P])
-            for c in range(S // P):
-                cols = slice(P * c, P * (c + 1))
-                nc.tensor.matmul(turned[:, c, :], lim_t[n][:, cols], ident[:], start=True, stop=False, is_transpose=True)
-                nc.tensor.matmul(turned[:, c, :], a_sb[n][:, cols], ident[:], start=False, stop=True, is_transpose=True)
+            chunks = S // P
+            for k, term in enumerate((lim_t[n], a_sb[n])):
+                for c in range(chunks):
+                    nc.tensor.matmul(
+                        turned[:, c, :],
+                        term[:, P * c : P * (c + 1)],
+                        ident[:],
+                        start=(k == 0 and c == 0),
+                        stop=(k == 1 and c == chunks - 1),
+                        is_transpose=True,
+                    )
             turned_t[n] = turned
 
         def turn_back(n):
@@ -286,7 +291,7 @@ def tile_list_vanilla_page_scores_kernel(
             if n < TILES - 2:
                 u = ring.tile([P, NP], F32, name="u", tag="step", bufs=1, align_bytes=64)
             else:
-                u = ring.tile([P, NP], F32, name="u_last", tag="lim", bufs=3)
+                u = ring.tile([P, NP], F32, name="u_last", tag="lim")
             nc.vector.tensor_scalar(
                 out=u[:],
                 in0=picked[n][:],
@@ -311,8 +316,8 @@ def tile_list_vanilla_page_scores_kernel(
         def weave_x(b, n):
             x_bf[b] = slot(n, [P, NP, PACK], BF16, "x_bf")
             nc.scalar.copy(
-                out=x_bf[b][:],
-                in_=x_planes[b][:].rearrange("p t c -> p c t"),
+                out=x_bf[b][:].rearrange("p (c i) t -> p c t i", i=4),
+                in_=x_planes[b][:].rearrange("p t (c i) -> p c t i", i=4),
             )
 
         x_codes, x_scales, page_codes, page_scales = {}, {}, {}, {}
@@ -335,8 +340,8 @@ def tile_list_vanilla_page_scores_kernel(
                 page_bf[b, 0], page_bf[b, 1] = whole[:, 0], whole[:, 1]
             src = staged[b][:, 0:planes, HALF * half : HALF * (half + 1)]
             nc.scalar.copy(
-                out=page_bf[b, half][:, :, 0:planes],
-                in_=src.rearrange("p t c -> p c t"),
+                out=page_bf[b, half].rearrange("p (c i) t -> p c t i", i=4)[:, :, 0:planes, :],
+                in_=src.rearrange("p t (c i) -> p c t i", i=4),
             )
 
         def quant_page(b, half):
@@ -434,8 +439,11 @@ def tile_list_vanilla_page_scores_kernel(
                 )
         for m in range(M_TILES):
             half, c = divmod(m, M_TILES // 2)
-            y = ring.tile([P, NP], F32, name="y", tag="lim", bufs=3)
-            nc.vector.tensor_tensor(out=y[:], in0=scores[m][:], in1=due_t[half][:, c, :], op=ALU.subtract)
+            y = slot(3 + m % 4, [P, NP], F32, "y")
             res = ring.tile([P, NP], F32, name="res", tag="page", bufs=6)
-            nc.scalar.activation(out=res[:], in_=y[:], func=ACT.Silu)
-            nc.sync.dma_start(out=out[P * m : P * (m + 1), :], in_=res[:])
+            pieces = 2 if m == M_TILES - 1 else 1
+            for k in range(pieces):
+                cols = slice(NP // pieces * k, NP // pieces * (k + 1))
+                nc.vector.tensor_tensor(out=y[:, cols], in0=scores[m][:, cols], in1=due_t[half][:, c, cols], op=ALU.subtract)
+                nc.scalar.activation(out=res[:, cols], in_=y[:, cols], func=ACT.Silu)
+                nc.sync.dma_start(out=out[P * m : P * (m + 1), cols], in_=res[:, cols])

@@ -21,15 +21,29 @@ P = 128
 PACK = 4
 KP = P * PACK
 A_PASSES = K // KP
-R_PASSES = H // KP
-TILES = R_PASSES * PACK
+GROUPS = H // KP
+LAST_GROUP = GROUPS - 1
+TILES = GROUPS * PACK
+LAST_TILE = TILES - 1
 M_TILES = T2 // P
+HALF = T2 // 2
 QUAD = 32
-AHEAD = 2
-PAGE_AHEAD = 4
+BLOCKS = P // 8
+LIST_ROWS = 16
+LINE = 4
+ALIGN = 64
+W1_SHAPE = [P, PACK, P, PACK]
 RING_BANKS = 4
+
+SUM_AHEAD = 2
+X_BEHIND = 2
+LIM_AHEAD = 2 * SUM_AHEAD
+PAGE_AHEAD = 4
+PAGE_BUFS = PAGE_AHEAD + 2
+W1_RAW_BUFS = 3
 VECTOR_M = 36
-W1_BF = [P, PACK, P, PACK]
+Y_BUFS = 4
+LAST_CAST_STEP = PACK * (LAST_GROUP - 1) + A_PASSES - 1
 
 
 def tile_list_vanilla_page_scores_kernel(
@@ -42,116 +56,110 @@ def tile_list_vanilla_page_scores_kernel(
         ring = ctx.enter_context(tc.tile_pool(name="ring", bufs=2))
         psum = ctx.enter_context(tc.psum_pool(name="psum", bufs=1))
 
+
         def bank(i, shape):
             return psum.tile(shape, F32, name="bank%d" % i, tag="bank%d" % i)
 
-        def slot(n, shape, dtype, name):
-            return keep.tile(shape, dtype, name=name, tag="slot%d" % n, align_bytes=64)
+        def after_a(n, shape, dtype, name):
+            return keep.tile(shape, dtype, name=name, tag="slot%d" % n, align_bytes=ALIGN)
 
-        def turn(n, shape, dtype, name):
-            return keep.tile(shape, dtype, name=name, tag="turn%d" % (n % 2), align_bytes=64)
+        def woven(n, shape, name):
+            return keep.tile(shape, BF16, name=name, tag="turn%d" % (n % 2), align_bytes=ALIGN)
 
-        idx1 = lists.tile([P, S // 16], U16)
-        idx2 = lists.tile([P, S // 16], U16)
-        idx3 = lists.tile([P, NP // 16], U16)
+        def in_step(shape, dtype, name):
+            return ring.tile(shape, dtype, name=name, tag="step", bufs=1, align_bytes=ALIGN)
+
+        idx1 = lists.tile([P, S // LIST_ROWS], U16)
+        idx2 = lists.tile([P, S // LIST_ROWS], U16)
+        idx3 = lists.tile([P, NP // LIST_ROWS], U16)
         nc.sync.dma_start(idx1[:], offs)
-        w4_raw = [keep.tile([P, 2 * H], U8, name="w4_raw%d" % a, align_bytes=64) for a in range(A_PASSES)]
+        w4_raw = [keep.tile([P, 2 * H], U8, name="w4_raw%d" % a, align_bytes=ALIGN) for a in range(A_PASSES)]
         for a in range(A_PASSES):
             nc.sync.dma_start(out=w4_raw[a][:].bitcast(I32), in_=w4_words[a].bitcast(I32))
-        tab_sc = keep.tile([P, A_PASSES, T], U8, align_bytes=64)
-        w4_sc = keep.tile([P, A_PASSES, H], U8, align_bytes=64)
+        tab_sc = keep.tile([P, A_PASSES, T], U8, align_bytes=ALIGN)
+        w4_sc = keep.tile([P, A_PASSES, H], U8, align_bytes=ALIGN)
         nc.gpsimd.memset(w4_sc[:].rearrange("p a n -> p (a n)").bitcast(I32), 0)
         nc.vector.memset(tab_sc[:].rearrange("p a n -> p (a n)").bitcast(I32), 0)
 
-        tab = []
+        tab, w1_raw, lim_t, page_t, weight_t = [], {}, {}, {}, {}
 
         def load_tab(a):
-            words = ring.tile([P, T], I32, name="tab", tag="staged", align_bytes=64)
+            words = ring.tile([P, T], I32, name="tab", tag="staged", align_bytes=ALIGN)
             nc.sync.dma_start(out=words[:], in_=tab_words[a].rearrange("p n i -> p (n i)").bitcast(I32))
             tab.append(words)
 
-        def load_scale_rows(plane, rows, q):
-            nc.gpsimd.dma_start(
-                out=plane[q:P:QUAD, :, :].bitcast(I32),
-                in_=rows[:, q:16:4, :].rearrange("a q n -> q a n").bitcast(I32),
-            )
+        def load_scale_planes(plane, rows):
+            for j in range(PACK):
+                nc.gpsimd.dma_start(
+                    out=plane[j:P:QUAD, :, :].bitcast(I32),
+                    in_=rows[:, j:BLOCKS:PACK, :].rearrange("a q n -> q a n").bitcast(I32),
+                )
 
-        w1_raw = {}
-
-        def load_w1(b, a, pieces=1):
+        def load_w1(b, a, pieces):
             width = KP // pieces
-            raw = ring.tile([P, pieces, PACK, width], F32, name="w1_raw", bufs=3)
+            raw = ring.tile([P, pieces, PACK, width], F32, name="w1_raw", bufs=W1_RAW_BUFS)
             for k in range(pieces):
                 rows = w1[KP * a : KP * (a + 1), KP * b + width * k : KP * b + width * (k + 1)]
-                nc.sync.dma_start(out=raw[:, k], in_=rows.rearrange("(p j) c -> p j c", j=PACK))
+                nc.sync.dma_start(out=raw[:, k], in_=rows.rearrange("(p i) c -> p i c", i=PACK))
             w1_raw[a, b] = raw
 
-        lim_t, page_t = {}, {}
+        def group_rows(x, b):
+            return x[KP * b : KP * (b + 1), :].rearrange("(p t) c -> p t c", t=PACK)
 
-        def rows_of(x, n):
-            b, t = divmod(n, PACK)
-            return x[KP * b : KP * (b + 1), :].rearrange("(p t) c -> p t c", t=PACK)[:, t, :]
-
-        def load_lim(n):
+        def load_lim(n, queue):
             b, t = divmod(n, PACK)
             pair = ring.tile([P, 2, S], F32, name="lim")
-            rows = lim[KP * b : KP * (b + 1), :].rearrange("(p t) c -> p t c", t=PACK)
-            (nc.sync if n < PACK else nc.scalar).dma_start(out=pair[:], in_=rows[:, t : t + 2, :])
+            queue.dma_start(out=pair[:], in_=group_rows(lim, b)[:, t : t + 2, :])
             lim_t[n], lim_t[n + 1] = pair[:, 0, :], pair[:, 1, :]
 
         def load_page(n):
-            page_t[n] = ring.tile([P, T2], F32, name="page", bufs=6)
-            nc.sync.dma_start(out=page_t[n][:], in_=rows_of(page0, n))
-
-        wgs_v = wgs.rearrange("(p t) j -> p t j", t=PACK)
-        weight_t = {}
+            b, t = divmod(n, PACK)
+            page_t[n] = ring.tile([P, T2], F32, name="page", bufs=PAGE_BUFS)
+            nc.sync.dma_start(out=page_t[n][:], in_=group_rows(page0, b)[:, t, :])
 
         def load_wgs(t0, t1, queue):
             planes = keep.tile([P, t1 - t0, S], F32, name="wgs%d" % t0)
+            rows = wgs.rearrange("(p t) j -> p t j", t=PACK)
             for q in range(P // QUAD):
-                queue.dma_start(out=planes[QUAD * q : QUAD * (q + 1), :, :], in_=wgs_v[:, t0:t1, :])
+                queue.dma_start(out=planes[QUAD * q : QUAD * (q + 1), :, :], in_=rows[:, t0:t1, :])
             for t in range(t0, t1):
                 weight_t[t] = planes[:, t - t0, :]
 
         load_wgs(0, 2, nc.scalar)
         row_consts = []
-        for name, v in (("cen", cen), ("cap", cap), ("vec", vec)):
-            cols = keep.tile([P, R_PASSES, PACK], F32, name=name)
-            nc.scalar.dma_start(out=cols[:], in_=v.rearrange("(b p t) -> p b t", p=P, t=PACK))
+        for name, values in (("cen", cen), ("cap", cap), ("vec", vec)):
+            cols = keep.tile([P, GROUPS, PACK], F32, name=name)
+            nc.scalar.dma_start(out=cols[:], in_=values.rearrange("(b p t) -> p b t", p=P, t=PACK))
             row_consts.append(cols)
         cen_c, cap_c, vec_c = row_consts
-        warm = keep.tile([P, 1], F32)
-        nc.scalar.activation(out=warm[:], in_=weight_t[0][:, 0:1], func=ACT.Silu)
-        for q in range(4):
-            load_scale_rows(w4_sc, w4_scales, q)
-        for q in range(4):
-            load_scale_rows(tab_sc, tab_scales, q)
-        load_tab(0)
-        load_w1(0, 0)
-        load_tab(1)
-        load_w1(0, 1, 2)
-        load_lim(0)
+        load_scale_planes(w4_sc, w4_scales)
+        load_scale_planes(tab_sc, tab_scales)
+        for a in range(A_PASSES):
+            load_tab(a)
+            load_w1(0, a, 2 if a == A_PASSES - 1 else 1)
+        load_lim(0, nc.sync)
         nc.sync.dma_start(idx2[:], offs2)
         load_page(0)
         nc.sync.dma_start(idx3[:], offs3)
-        load_lim(2)
-        load_w1(1, 0)
-        load_page(1)
-        load_w1(1, 1)
-        load_wgs(2, 3, nc.sync)
-        load_page(2)
-        load_wgs(3, 4, nc.sync)
-        load_page(3)
+        load_lim(SUM_AHEAD, nc.sync)
+        for n in range(PAGE_AHEAD):
+            if n >= 2:
+                load_wgs(n, n + 1, nc.sync)
+            if n >= 1:
+                load_page(n)
+            if n < A_PASSES:
+                load_w1(1, n, 1)
 
         ident = keep.tile([P, P], F32)
         make_identity(nc, ident[:])
-        w4_dealt = keep.tile([P, A_PASSES * R_PASSES, PACK, 2 * P], U8, align_bytes=64)
+
+        w4_dealt = keep.tile([P, A_PASSES * GROUPS, PACK, 2 * P], U8, align_bytes=ALIGN)
         for a in range(A_PASSES):
             nc.vector.tensor_copy(
-                out=w4_dealt[:, R_PASSES * a : R_PASSES * (a + 1)].bitcast(U16).rearrange("p b t m -> p t b m"),
+                out=w4_dealt[:, GROUPS * a : GROUPS * (a + 1)].bitcast(U16).rearrange("p b t m -> p t b m"),
                 in_=w4_raw[a][:].bitcast(U16).rearrange("p (b m t) -> p t b m", m=P, t=PACK),
             )
-        w4_sc_dealt = keep.tile([P, A_PASSES * R_PASSES, PACK, P], U8, align_bytes=64)
+        w4_sc_dealt = keep.tile([P, A_PASSES * GROUPS, PACK, P], U8, align_bytes=ALIGN)
         nc.vector.tensor_copy(
             out=w4_sc_dealt[:],
             in_=w4_sc[:].rearrange("p a n -> p (a n)").rearrange("p (g m t) -> p g t m", m=P, t=PACK),
@@ -159,45 +167,54 @@ def tile_list_vanilla_page_scores_kernel(
 
         v_words, v_scales = [], []
         for a in range(A_PASSES):
-            sc = keep.tile([P, S], U8, name="v_scales%d" % a, align_bytes=64)
-            nc.vector.tensor_copy(out=sc[:], in_=tab_sc[:, a, :].indirect(idx1[:]))
-            v_scales.append(sc)
+            picked_scales = keep.tile([P, S], U8, name="v_scales%d" % a, align_bytes=ALIGN)
+            nc.vector.tensor_copy(out=picked_scales[:], in_=tab_sc[:, a, :].indirect(idx1[:]))
+            v_scales.append(picked_scales)
         for a in range(A_PASSES):
-            words = keep.tile([P, S], I32, name="v_words%d" % a, align_bytes=64)
-            nc.vector.tensor_copy(out=words[:].bitcast(U32), in_=tab[a][:].bitcast(U32).indirect(idx1[:]))
-            v_words.append(words)
+            picked_words = keep.tile([P, S], I32, name="v_words%d" % a, align_bytes=ALIGN)
+            nc.vector.tensor_copy(out=picked_words[:].bitcast(U32), in_=tab[a][:].bitcast(U32).indirect(idx1[:]))
+            v_words.append(picked_words)
 
-        w1_bf, w1_codes, w1_scales = {}, {}, {}
+        w1_codes, w1_scales = {}, {}
 
-        def cast_w1(a, b, grouped):
-            w1_bf[a, b] = grouped
-            dst = grouped[:].rearrange("p t m j -> p m j t")
-            if (a, b) != (A_PASSES - 1, 0):
-                nc.scalar.copy(out=dst, in_=w1_raw[a, b][:, 0].rearrange("p j (m t) -> p m j t", t=PACK))
-                return
-            half = P // 2
-            early, late = [w1_raw[a, b][:, k].rearrange("p j (m t) -> p m j t", t=PACK) for k in range(2)]
-            nc.scalar.copy(out=dst[:, 0:half], in_=early)
-            nc.vector.tensor_copy(out=dst[:, half : half + VECTOR_M], in_=late[:, 0:VECTOR_M])
-            nc.scalar.copy(out=dst[:, half + VECTOR_M : P], in_=late[:, VECTOR_M:half])
+        def w1_source(a, b, piece):
+            return w1_raw[a, b][:, piece].rearrange("p i (m t) -> p m i t", t=PACK)
 
-        def quant_w1(a, b, spans):
-            codes = ring.tile([P, KP], U32, name="w1_codes", bufs=4, align_bytes=64)
-            scales = ring.tile([P, KP], U8, name="w1_scales", bufs=4, align_bytes=64)
+        def w1_target(dealt):
+            return dealt[:].rearrange("p t m i -> p m i t")
+
+        def quant_w1(a, b, dealt, spans):
+            codes = ring.tile([P, KP], U32, name="w1_codes", bufs=2 * A_PASSES, align_bytes=ALIGN)
+            scales = ring.tile([P, KP], U8, name="w1_scales", bufs=2 * A_PASSES, align_bytes=ALIGN)
             for t0, t1 in spans:
                 nc.vector.quantize_mx(
                     out=codes[:, P * t0 : P * t1].bitcast(FP8X4),
                     scales=scales[:, P * t0 : P * t1],
-                    in_=w1_bf[a, b][:, t0:t1].rearrange("p t m j -> p (t m j)"),
+                    in_=dealt[:, t0:t1].rearrange("p t m i -> p (t m i)"),
                 )
             w1_codes[a, b], w1_scales[a, b] = codes, scales
 
-        def first_product(n):
+        def prepare_w1(a, b, dealt):
+            nc.scalar.copy(out=w1_target(dealt), in_=w1_source(a, b, 0))
+            quant_w1(a, b, dealt, [(0, PACK)])
+
+        def prepare_last_loaded_w1():
+            a, mid = A_PASSES - 1, P // 2
+            dealt = woven(a, W1_SHAPE, "w1_bf")
+            target = w1_target(dealt)
+            nc.scalar.copy(out=target[:, 0:mid], in_=w1_source(a, 0, 0))
+            nc.vector.tensor_copy(out=target[:, mid : mid + VECTOR_M], in_=w1_source(a, 0, 1)[:, 0:VECTOR_M])
+            nc.scalar.copy(out=target[:, mid + VECTOR_M : P], in_=w1_source(a, 0, 1)[:, VECTOR_M:mid])
+            quant_w1(a, 0, dealt, [(0, 1), (1, 2), (2, PACK)])
+
+        a_sb, turned_t, half_sum = {}, {}, {}
+
+        def first_product(n, bank_index):
             b, t = divmod(n, PACK)
-            acc = bank((n + 2) % RING_BANKS if n > 0 else 0, [P, S])
+            acc = bank(bank_index, [P, S])
             cols = slice(P * t, P * (t + 1))
             for a in range(A_PASSES):
-                g = R_PASSES * a + b
+                g = GROUPS * a + b
                 nc.tensor.matmul_mx(
                     out=acc[:],
                     lhsT=w4_dealt[:, g, t, :].bitcast(FP4X4),
@@ -219,46 +236,45 @@ def tile_list_vanilla_page_scores_kernel(
                 )
             return acc
 
-        a_sb, half_sum = {}, {}
-
-        turned_t = {}
-
-        def front(n):
-            acc = first_product(n)
-            a_sb[n] = slot(n, [P, S], F32, "a_sb")
+        def start_sum(n):
+            acc = first_product(n, (n - SUM_AHEAD) % RING_BANKS)
+            a_sb[n] = after_a(n, [P, S], F32, "a_sb")
             nc.scalar.copy(out=a_sb[n][:], in_=acc[:])
-            turned = bank(RING_BANKS + n % RING_BANKS, [P, S // P, P])
             chunks = S // P
+            turned_t[n] = bank(RING_BANKS + n % RING_BANKS, [P, chunks, P])
             for k, term in enumerate((lim_t[n], a_sb[n])):
                 for c in range(chunks):
                     nc.tensor.matmul(
-                        turned[:, c, :],
+                        turned_t[n][:, c, :],
                         term[:, P * c : P * (c + 1)],
                         ident[:],
                         start=(k == 0 and c == 0),
                         stop=(k == 1 and c == chunks - 1),
                         is_transpose=True,
                     )
-            turned_t[n] = turned
 
-        def turn_back(n):
-            turned = turned_t[n]
-            turned_sb = ring.tile([P, S // P, P], F32, name="turned_sb", tag="step", bufs=1, align_bytes=64)
-            nc.scalar.activation(out=turned_sb[:], in_=turned[:], func=ACT.Copy, scale=0.5)
+        def finish_sum(n):
+            turned_sb = in_step([P, S // P, P], F32, "turned_sb")
+            nc.scalar.activation(out=turned_sb[:], in_=turned_t[n][:], func=ACT.Copy, scale=0.5)
             half_sum[n] = bank(n % RING_BANKS, [P, S // P, P])
             for c in range(S // P):
                 nc.tensor.transpose(half_sum[n][:, c, :], turned_sb[:, c, :], ident[:])
 
-        def make_h(n):
-            h = keep.tile([P, S], F32, name="h", tag="h")
-            if n == 0:
-                acc = first_product(0)
-                total = ring.tile([P, S], F32, name="total", tag="step", bufs=1, align_bytes=64)
-                nc.vector.scalar_tensor_tensor(
-                    out=total[:], in0=acc[:], scalar=0.5, in1=half_lim[:], op0=ALU.mult, op1=ALU.add
-                )
-                nc.vector.scalar_tensor_tensor(out=h[:], in0=acc[:], scalar=0.0, in1=total[:], op0=ALU.max, op1=ALU.min)
-                return h
+        def half_h_tile():
+            return keep.tile([P, S], F32, name="h", tag="h")
+
+        def first_half_h():
+            h = half_h_tile()
+            acc = first_product(0, 0)
+            total = in_step([P, S], F32, "total")
+            nc.vector.scalar_tensor_tensor(
+                out=total[:], in0=acc[:], scalar=0.5, in1=half_lim[:], op0=ALU.mult, op1=ALU.add
+            )
+            nc.vector.scalar_tensor_tensor(out=h[:], in0=acc[:], scalar=0.0, in1=total[:], op0=ALU.max, op1=ALU.min)
+            return h
+
+        def half_h(n):
+            h = half_h_tile()
             nc.vector.scalar_tensor_tensor(
                 out=h[:],
                 in0=a_sb[n][:],
@@ -269,31 +285,35 @@ def tile_list_vanilla_page_scores_kernel(
             )
             return h
 
+        def double_wgs(t):
+            nc.scalar.mul(out=weight_t[t], in_=weight_t[t], mul=2.0)
+
         staged, page_bf, x_planes, x_bf, picked = {}, {}, {}, {}, {}
-        last = R_PASSES - 1
+        x_codes, x_scales, page_codes, page_scales = {}, {}, {}, {}
+
+        def scatter(n, h):
+            nc.vector.tensor_tensor(
+                out=page_t[n][:].indirect(idx2[:]), in0=h[:], in1=weight_t[n % PACK], op=ALU.mult
+            )
 
         def gather(n):
             picked[n] = ring.tile([P, NP], F32, name="picked", bufs=1)
             nc.vector.tensor_copy(out=picked[n][:], in_=page_t[n][:].indirect(idx3[:]))
 
-        def scatter(n, h):
-            b, t = divmod(n, PACK)
-            nc.vector.tensor_tensor(out=page_t[n][:].indirect(idx2[:]), in0=h[:], in1=weight_t[t], op=ALU.mult)
-
         def stage(n):
             b, t = divmod(n, PACK)
             if t == 0:
-                staged[b] = ring.tile([P, PACK, T2], F32, name="staged", align_bytes=64)
+                staged[b] = ring.tile([P, PACK, T2], F32, name="staged", align_bytes=ALIGN)
             nc.sync.dma_start(out=staged[b][:, t, :], in_=page_t[n][:])
 
         def make_x(n):
             b, t = divmod(n, PACK)
-            if n < TILES - 2:
-                u = ring.tile([P, NP], F32, name="u", tag="step", bufs=1, align_bytes=64)
+            if n < TILES - X_BEHIND:
+                capped = in_step([P, NP], F32, "u")
             else:
-                u = ring.tile([P, NP], F32, name="u_last", tag="lim")
+                capped = ring.tile([P, NP], F32, name="u_last", tag="lim")
             nc.vector.tensor_scalar(
-                out=u[:],
+                out=capped[:],
                 in0=picked[n][:],
                 scalar1=cen_c[:, b, t : t + 1],
                 scalar2=cap_c[:, b, t : t + 1],
@@ -301,130 +321,121 @@ def tile_list_vanilla_page_scores_kernel(
                 op1=ALU.min,
             )
             factor = vec_c[:, b, t : t + 1]
-            if b < last:
+            if b < LAST_GROUP:
                 if t == 0:
                     x_planes[b] = ring.tile([P, PACK, NP], BF16, name="x_planes")
-                nc.scalar.activation(out=x_planes[b][:, t, :], in_=u[:], func=ACT.Copy, scale=factor)
+                nc.scalar.activation(out=x_planes[b][:, t, :], in_=capped[:], func=ACT.Copy, scale=factor)
+                return
+            if t == 0:
+                x_bf[b] = ring.tile([P, NP, PACK], BF16, name="x_last", bufs=1, align_bytes=ALIGN)
+            if t < PACK // 2:
+                nc.scalar.activation(out=x_bf[b][:, :, t], in_=capped[:], func=ACT.Copy, scale=factor)
             else:
-                if t == 0:
-                    x_bf[b] = ring.tile([P, NP, PACK], BF16, name="x_last", bufs=1, align_bytes=64)
-                if t < 2:
-                    nc.scalar.activation(out=x_bf[b][:, :, t], in_=u[:], func=ACT.Copy, scale=factor)
-                else:
-                    nc.vector.tensor_scalar(out=x_bf[b][:, :, t], in0=u[:], scalar1=factor, scalar2=None, op0=ALU.mult)
+                nc.vector.tensor_scalar(out=x_bf[b][:, :, t], in0=capped[:], scalar1=factor, scalar2=None, op0=ALU.mult)
+
 
         def weave_x(b, n):
-            x_bf[b] = slot(n, [P, NP, PACK], BF16, "x_bf")
+            x_bf[b] = after_a(n, [P, NP, PACK], BF16, "x_bf")
             nc.scalar.copy(
-                out=x_bf[b][:].rearrange("p (c i) t -> p c t i", i=4),
-                in_=x_planes[b][:].rearrange("p t (c i) -> p c t i", i=4),
+                out=x_bf[b][:].rearrange("p (c i) t -> p c t i", i=LINE),
+                in_=x_planes[b][:].rearrange("p t (c i) -> p c t i", i=LINE),
             )
 
-        x_codes, x_scales, page_codes, page_scales = {}, {}, {}, {}
+        def weave_page(b, half, tiles):
+            nc.scalar.copy(
+                out=page_bf[b, half].rearrange("p (c i) t -> p c t i", i=LINE)[:, :, 0:tiles, :],
+                in_=staged[b][:, 0:tiles, HALF * half : HALF * (half + 1)].rearrange("p t (c i) -> p c t i", i=LINE),
+            )
 
-        def quant_x(b, n):
-            x_codes[b] = slot(n, [P, NP], U32, "x_codes")
-            x_scales[b] = keep.tile([P, NP], U8, name="x_scales%d" % b, align_bytes=64)
+        def quant_x(b, buffer):
+            x_codes[b] = after_a(buffer, [P, NP], U32, "x_codes")
+            x_scales[b] = keep.tile([P, NP], U8, name="x_scales%d" % b, align_bytes=ALIGN)
             nc.vector.quantize_mx(
                 out=x_codes[b][:].bitcast(FP8X4), scales=x_scales[b][:], in_=x_bf[b][:].rearrange("p c t -> p (c t)")
             )
 
-        HALF = T2 // 2
-
-        def weave_page(b, half, planes, n):
-            if b < last:
-                piece = turn(n, [P, HALF, PACK], BF16, "page_bf")
-                page_bf[b, half] = piece[:]
-            elif half == 0:
-                whole = ring.tile([P, 2, HALF, PACK], BF16, name="page_last", tag="step", bufs=1, align_bytes=64)
-                page_bf[b, 0], page_bf[b, 1] = whole[:, 0], whole[:, 1]
-            src = staged[b][:, 0:planes, HALF * half : HALF * (half + 1)]
-            nc.scalar.copy(
-                out=page_bf[b, half].rearrange("p (c i) t -> p c t i", i=4)[:, :, 0:planes, :],
-                in_=src.rearrange("p t (c i) -> p c t i", i=4),
-            )
-
         def quant_page(b, half):
-            codes = keep.tile([P, HALF], U32, name="page_codes%d_%d" % (b, half), align_bytes=64)
-            scales = keep.tile([P, HALF], U8, name="page_scales%d_%d" % (b, half), align_bytes=64)
+            codes = keep.tile([P, HALF], U32, name="page_codes%d_%d" % (b, half), align_bytes=ALIGN)
+            scales = keep.tile([P, HALF], U8, name="page_scales%d_%d" % (b, half), align_bytes=ALIGN)
             nc.vector.quantize_mx(
                 out=codes[:].bitcast(FP8X4), scales=scales[:], in_=page_bf[b, half].rearrange("p c t -> p (c t)")
             )
             page_codes[b, half], page_scales[b, half] = codes, scales
 
-        cast_w1(0, 0, turn(0, W1_BF, BF16, "w1_bf"))
-        quant_w1(0, 0, [(0, PACK)])
-        cast_w1(1, 0, turn(1, W1_BF, BF16, "w1_bf"))
-        quant_w1(1, 0, [(0, 1), (1, 2), (2, PACK)])
+        page_steps, x_steps = {}, {}
+        for b in range(LAST_GROUP):
+            first = max(PACK * (b + 1) + 1, LAST_CAST_STEP + 1)
+            page_steps[first], page_steps[first + 1] = (b, 0), (b, 1)
+            x_steps[first + 2 if first + 2 < LAST_TILE else first] = b
+
+        prepare_w1(0, 0, woven(0, W1_SHAPE, "w1_bf"))
+        prepare_last_loaded_w1()
         half_lim = keep.tile([P, S], F32)
         nc.scalar.mul(out=half_lim[:], in_=lim_t[0], mul=0.5)
-        nc.scalar.mul(out=weight_t[0], in_=weight_t[0], mul=2.0)
-
-        def weave_last_plane(t, half):
-            cols = slice(HALF * half, HALF * (half + 1))
-            nc.scalar.copy(out=page_bf[last, half][:, :, t], in_=page_t[PACK * last + t][:, cols])
-
-        w1_steps = {0: (0, 1), 1: (1, 1), 4: (0, 2), 5: (1, 2)}
-        page_steps = {6: (0, 0), 7: (0, 1), 9: (1, 0), 10: (1, 1)}
-        x_steps = {8: 0, 9: 1}
+        double_wgs(0)
 
         due_t = []
         for n in range(TILES):
             b, t = divmod(n, PACK)
-            if n >= 2:
-                make_x(n - 2)
-            h = make_h(n)
+            if n >= X_BEHIND:
+                make_x(n - X_BEHIND)
+            h = first_half_h() if n == 0 else half_h(n)
             if n >= 1:
                 gather(n - 1)
-            if n == TILES - 1:
-                quant_x(0, TILES - 1)
+            if n == LAST_TILE:
+                quant_x(0, LAST_TILE)
                 quant_x(1, 1)
             scatter(n, h)
             if n == 0:
-                front(1)
+                start_sum(1)
             if n + 1 < PACK:
-                nc.scalar.mul(out=weight_t[n + 1], in_=weight_t[n + 1], mul=2.0)
+                double_wgs(n + 1)
             if n + 1 < TILES:
-                turn_back(n + 1)
-            if n + AHEAD < TILES:
-                front(n + AHEAD)
-            if n % 2 == 0 and n + 4 < TILES:
-                load_lim(n + 4)
+                finish_sum(n + 1)
+            if n + SUM_AHEAD < TILES:
+                start_sum(n + SUM_AHEAD)
+            if n % 2 == 0 and n + LIM_AHEAD < TILES:
+                load_lim(n + LIM_AHEAD, nc.scalar)
             if n + PAGE_AHEAD < TILES:
                 load_page(n + PAGE_AHEAD)
-            if n in (0, 1):
-                load_w1(2, n)
-            if n < TILES - 1:
+            if n < A_PASSES:
+                load_w1(LAST_GROUP, n, 1)
+            if n < LAST_TILE:
                 stage(n)
-            if n in w1_steps:
-                a, group = w1_steps[n]
-                cast_w1(a, group, turn(n, W1_BF, BF16, "w1_bf") if n > 0 else slot(0, W1_BF, BF16, "w1_bf"))
-                quant_w1(a, group, [(0, PACK)])
+            if b < LAST_GROUP and t < A_PASSES:
+                dealt = after_a(0, W1_SHAPE, BF16, "w1_bf") if n == 0 else woven(n, W1_SHAPE, "w1_bf")
+                prepare_w1(t, b + 1, dealt)
             if n in page_steps:
                 group, half = page_steps[n]
-                weave_page(group, half, PACK, n)
+                page_bf[group, half] = woven(n, [P, HALF, PACK], "page_bf")[:]
+                weave_page(group, half, PACK)
                 quant_page(group, half)
             if n in x_steps:
                 weave_x(x_steps[n], n)
-            if n in (6, 7):
-                d = ring.tile([P, M_TILES // 2, NP], F32, name="due", tag="w1_raw", bufs=3)
-                rows = due[HALF * (n - 6) : HALF * (n - 5), :]
-                nc.sync.dma_start(out=d[:], in_=rows.rearrange("(i p) j -> p i j", p=P))
-                due_t.append(d)
+            if LAST_CAST_STEP < n <= LAST_CAST_STEP + 2:
+                k = n - LAST_CAST_STEP - 1
+                due_half = ring.tile([P, M_TILES // 2, NP], F32, name="due", tag="w1_raw", bufs=W1_RAW_BUFS)
+                rows = due[HALF * k : HALF * (k + 1), :]
+                nc.sync.dma_start(out=due_half[:], in_=rows.rearrange("(i p) j -> p i j", p=P))
+                due_t.append(due_half)
 
-        make_x(TILES - 2)
-        gather(TILES - 1)
+        make_x(LAST_TILE - 1)
+        gather(LAST_TILE)
+        page_last = in_step([P, 2, HALF, PACK], BF16, "page_last")
         for half in range(2):
-            weave_page(last, half, PACK - 1, TILES)
+            page_bf[LAST_GROUP, half] = page_last[:, half]
+            weave_page(LAST_GROUP, half, PACK - 1)
         for half in range(2):
-            weave_last_plane(PACK - 1, half)
-        make_x(TILES - 1)
-        quant_page(last, 0)
-        quant_x(last, 2)
-        quant_page(last, 1)
+            nc.scalar.copy(
+                out=page_bf[LAST_GROUP, half][:, :, PACK - 1], in_=page_t[LAST_TILE][:, HALF * half : HALF * (half + 1)]
+            )
+        make_x(LAST_TILE)
+        quant_page(LAST_GROUP, 0)
+        quant_x(LAST_GROUP, LAST_GROUP)
+        quant_page(LAST_GROUP, 1)
 
         scores = [bank((m + RING_BANKS) % M_TILES, [P, NP]) for m in range(M_TILES)]
-        for b in range(R_PASSES):
+        for b in range(GROUPS):
             for m in range(M_TILES):
                 half, c = divmod(m, M_TILES // 2)
                 cols = slice(P * c, P * (c + 1))
@@ -435,15 +446,17 @@ def tile_list_vanilla_page_scores_kernel(
                     rhs=x_codes[b][:].bitcast(FP8X4),
                     rhs_scale=x_scales[b][:],
                     start=(b == 0),
-                    stop=(b == last),
+                    stop=(b == LAST_GROUP),
                 )
         for m in range(M_TILES):
             half, c = divmod(m, M_TILES // 2)
-            y = slot(3 + m % 4, [P, NP], F32, "y")
-            res = ring.tile([P, NP], F32, name="res", tag="page", bufs=6)
+            diff = after_a(GROUPS + m % Y_BUFS, [P, NP], F32, "y")
+            res = ring.tile([P, NP], F32, name="res", tag="page", bufs=PAGE_BUFS)
             pieces = 2 if m == M_TILES - 1 else 1
             for k in range(pieces):
                 cols = slice(NP // pieces * k, NP // pieces * (k + 1))
-                nc.vector.tensor_tensor(out=y[:, cols], in0=scores[m][:, cols], in1=due_t[half][:, c, cols], op=ALU.subtract)
-                nc.scalar.activation(out=res[:, cols], in_=y[:, cols], func=ACT.Silu)
+                nc.vector.tensor_tensor(
+                    out=diff[:, cols], in0=scores[m][:, cols], in1=due_t[half][:, c, cols], op=ALU.subtract
+                )
+                nc.scalar.activation(out=res[:, cols], in_=diff[:, cols], func=ACT.Silu)
                 nc.sync.dma_start(out=out[P * m : P * (m + 1), cols], in_=res[:, cols])

from contextlib import ExitStack

import concourse.mybir as mybir
from concourse.masks import make_identity

K, H, T, S, T2, NP = 1024, 1536, 2048, 512, 1024, 512
FLOPS = 2 * (2 * K * H * S + H * T2 * NP)

F32 = mybir.dt.float32
BF16 = mybir.dt.bfloat16
I32 = mybir.dt.int32
U32 = mybir.dt.uint32
U16 = mybir.dt.uint16
U8 = mybir.dt.uint8
FP8X4 = mybir.dt.float8_e4m3fn_x4
FP4X4 = mybir.dt.float4_e2m1fn_x4
ALU = mybir.AluOpType
ACT = mybir.ActivationFunctionType

P = 128
PACK = 4
KP = P * PACK
A_PASSES = K // KP
GROUPS = H // KP
LAST_GROUP = GROUPS - 1
TILES = GROUPS * PACK
LAST_TILE = TILES - 1
M_TILES = T2 // P
HALF = T2 // 2
QUAD = 32
BLOCKS = P // 8
LIST_ROWS = 16
LINE = 4
ALIGN = 64
W1_SHAPE = [P, PACK, P, PACK]
RING_BANKS = 4

SUM_AHEAD = 2
X_BEHIND = 2
LIM_AHEAD = 2 * SUM_AHEAD
PAGE_AHEAD = 4
PAGE_BUFS = PAGE_AHEAD + 2
W1_RAW_BUFS = 3
VECTOR_M = 36
Y_BUFS = 4
LAST_CAST_STEP = PACK * (LAST_GROUP - 1) + A_PASSES - 1


def tile_list_vanilla_page_scores_kernel(
    tc, tab_words, tab_scales, w4_words, w4_scales, w1, lim, wgs, page0, cen, cap, vec, due, offs, offs2, offs3, out
):
    nc = tc.nc
    with ExitStack() as ctx:
        lists = ctx.enter_context(tc.tile_pool(name="lists", bufs=1))
        keep = ctx.enter_context(tc.tile_pool(name="keep", bufs=1))
        ring = ctx.enter_context(tc.tile_pool(name="ring", bufs=2))
        psum = ctx.enter_context(tc.psum_pool(name="psum", bufs=1))


        def bank(i, shape):
            return psum.tile(shape, F32, name="bank%d" % i, tag="bank%d" % i)

        def after_a(n, shape, dtype, name):
            return keep.tile(shape, dtype, name=name, tag="slot%d" % n, align_bytes=ALIGN)

        def woven(n, shape, name):
            return keep.tile(shape, BF16, name=name, tag="turn%d" % (n % 2), align_bytes=ALIGN)

        def in_step(shape, dtype, name):
            return ring.tile(shape, dtype, name=name, tag="step", bufs=1, align_bytes=ALIGN)

        idx1 = lists.tile([P, S // LIST_ROWS], U16)
        idx2 = lists.tile([P, S // LIST_ROWS], U16)
        idx3 = lists.tile([P, NP // LIST_ROWS], U16)
        nc.sync.dma_start(idx1[:], offs)
        w4_raw = [keep.tile([P, 2 * H], U8, name="w4_raw%d" % a, align_bytes=ALIGN) for a in range(A_PASSES)]
        for a in range(A_PASSES):
            nc.sync.dma_start(out=w4_raw[a][:].bitcast(I32), in_=w4_words[a].bitcast(I32))
        tab_sc = keep.tile([P, A_PASSES, T], U8, align_bytes=ALIGN)
        w4_sc = keep.tile([P, A_PASSES, H], U8, align_bytes=ALIGN)
        nc.gpsimd.memset(w4_sc[:].rearrange("p a n -> p (a n)").bitcast(I32), 0)
        nc.vector.memset(tab_sc[:].rearrange("p a n -> p (a n)").bitcast(I32), 0)

        tab, w1_raw, lim_t, page_t, weight_t = [], {}, {}, {}, {}

        def load_tab(a):
            words = ring.tile([P, T], I32, name="tab", tag="staged", align_bytes=ALIGN)
            nc.sync.dma_start(out=words[:], in_=tab_words[a].rearrange("p n i -> p (n i)").bitcast(I32))
            tab.append(words)

        def load_scale_planes(plane, rows):
            for j in range(PACK):
                nc.gpsimd.dma_start(
                    out=plane[j:P:QUAD, :, :].bitcast(I32),
                    in_=rows[:, j:BLOCKS:PACK, :].rearrange("a q n -> q a n").bitcast(I32),
                )

        def load_w1(b, a, pieces):
            width = KP // pieces
            raw = ring.tile([P, pieces, PACK, width], F32, name="w1_raw", bufs=W1_RAW_BUFS)
            for k in range(pieces):
                rows = w1[KP * a : KP * (a + 1), KP * b + width * k : KP * b + width * (k + 1)]
                nc.sync.dma_start(out=raw[:, k], in_=rows.rearrange("(p i) c -> p i c", i=PACK))
            w1_raw[a, b] = raw

        def group_rows(x, b):
            return x[KP * b : KP * (b + 1), :].rearrange("(p t) c -> p t c", t=PACK)

        def load_lim(n, queue):
            b, t = divmod(n, PACK)
            pair = ring.tile([P, 2, S], F32, name="lim")
            queue.dma_start(out=pair[:], in_=group_rows(lim, b)[:, t : t + 2, :])
            lim_t[n], lim_t[n + 1] = pair[:, 0, :], pair[:, 1, :]

        def load_page(n):
            b, t = divmod(n, PACK)
            page_t[n] = ring.tile([P, T2], F32, name="page", bufs=PAGE_BUFS)
            nc.sync.dma_start(out=page_t[n][:], in_=group_rows(page0, b)[:, t, :])

        def load_wgs(t0, t1, queue):
            planes = keep.tile([P, t1 - t0, S], F32, name="wgs%d" % t0)
            rows = wgs.rearrange("(p t) j -> p t j", t=PACK)
            for q in range(P // QUAD):
                queue.dma_start(out=planes[QUAD * q : QUAD * (q + 1), :, :], in_=rows[:, t0:t1, :])
            for t in range(t0, t1):
                weight_t[t] = planes[:, t - t0, :]

        load_wgs(0, 2, nc.scalar)
        row_consts = []
        for name, values in (("cen", cen), ("cap", cap), ("vec", vec)):
            cols = keep.tile([P, GROUPS, PACK], F32, name=name)
            nc.scalar.dma_start(out=cols[:], in_=values.rearrange("(b p t) -> p b t", p=P, t=PACK))
            row_consts.append(cols)
        cen_c, cap_c, vec_c = row_consts
        load_scale_planes(w4_sc, w4_scales)
        load_scale_planes(tab_sc, tab_scales)
        for a in range(A_PASSES):
            load_tab(a)
            load_w1(0, a, 2 if a == A_PASSES - 1 else 1)
        load_lim(0, nc.sync)
        nc.sync.dma_start(idx2[:], offs2)
        load_page(0)
        nc.sync.dma_start(idx3[:], offs3)
        load_lim(SUM_AHEAD, nc.sync)
        for n in range(PAGE_AHEAD):
            if n >= 2:
                load_wgs(n, n + 1, nc.sync)
            if n >= 1:
                load_page(n)
            if n < A_PASSES:
                load_w1(1, n, 1)

        ident = keep.tile([P, P], F32)
        make_identity(nc, ident[:])

        w4_dealt = keep.tile([P, A_PASSES * GROUPS, PACK, 2 * P], U8, align_bytes=ALIGN)
        for a in range(A_PASSES):
            nc.vector.tensor_copy(
                out=w4_dealt[:, GROUPS * a : GROUPS * (a + 1)].bitcast(U16).rearrange("p b t m -> p t b m"),
                in_=w4_raw[a][:].bitcast(U16).rearrange("p (b m t) -> p t b m", m=P, t=PACK),
            )
        w4_sc_dealt = keep.tile([P, A_PASSES * GROUPS, PACK, P], U8, align_bytes=ALIGN)
        nc.vector.tensor_copy(
            out=w4_sc_dealt[:],
            in_=w4_sc[:].rearrange("p a n -> p (a n)").rearrange("p (g m t) -> p g t m", m=P, t=PACK),
        )

        v_words, v_scales = [], []
        for a in range(A_PASSES):
            picked_scales = keep.tile([P, S], U8, name="v_scales%d" % a, align_bytes=ALIGN)
            nc.vector.tensor_copy(out=picked_scales[:], in_=tab_sc[:, a, :].indirect(idx1[:]))
            v_scales.append(picked_scales)
        for a in range(A_PASSES):
            picked_words = keep.tile([P, S], I32, name="v_words%d" % a, align_bytes=ALIGN)
            nc.vector.tensor_copy(out=picked_words[:].bitcast(U32), in_=tab[a][:].bitcast(U32).indirect(idx1[:]))
            v_words.append(picked_words)

        w1_codes, w1_scales = {}, {}

        def w1_source(a, b, piece):
            return w1_raw[a, b][:, piece].rearrange("p i (m t) -> p m i t", t=PACK)

        def w1_target(dealt):
            return dealt[:].rearrange("p t m i -> p m i t")

        def quant_w1(a, b, dealt, spans):
            codes = ring.tile([P, KP], U32, name="w1_codes", bufs=2 * A_PASSES, align_bytes=ALIGN)
            scales = ring.tile([P, KP], U8, name="w1_scales", bufs=2 * A_PASSES, align_bytes=ALIGN)
            for t0, t1 in spans:
                nc.vector.quantize_mx(
                    out=codes[:, P * t0 : P * t1].bitcast(FP8X4),
                    scales=scales[:, P * t0 : P * t1],
                    in_=dealt[:, t0:t1].rearrange("p t m i -> p (t m i)"),
                )
            w1_codes[a, b], w1_scales[a, b] = codes, scales

        def prepare_w1(a, b, dealt):
            nc.scalar.copy(out=w1_target(dealt), in_=w1_source(a, b, 0))
            quant_w1(a, b, dealt, [(0, PACK)])

        def prepare_last_loaded_w1():
            a, mid = A_PASSES - 1, P // 2
            dealt = woven(a, W1_SHAPE, "w1_bf")
            target = w1_target(dealt)
            nc.scalar.copy(out=target[:, 0:mid], in_=w1_source(a, 0, 0))
            nc.vector.tensor_copy(out=target[:, mid : mid + VECTOR_M], in_=w1_source(a, 0, 1)[:, 0:VECTOR_M])
            nc.scalar.copy(out=target[:, mid + VECTOR_M : P], in_=w1_source(a, 0, 1)[:, VECTOR_M:mid])
            quant_w1(a, 0, dealt, [(0, 1), (1, 2), (2, PACK)])

        a_sb, turned_t, half_sum = {}, {}, {}

        def first_product(n, bank_index):
            b, t = divmod(n, PACK)
            acc = bank(bank_index, [P, S])
            cols = slice(P * t, P * (t + 1))
            for a in range(A_PASSES):
                g = GROUPS * a + b
                nc.tensor.matmul_mx(
                    out=acc[:],
                    lhsT=w4_dealt[:, g, t, :].bitcast(FP4X4),
                    lhsT_scale=w4_sc_dealt[:, g, t, :],
                    rhs=v_words[a][:].bitcast(FP8X4),
                    rhs_scale=v_scales[a][:],
                    start=(a == 0),
                    stop=False,
                )
            for a in range(A_PASSES):
                nc.tensor.matmul_mx(
                    out=acc[:],
                    lhsT=w1_codes[a, b][:, cols].bitcast(FP8X4),
                    lhsT_scale=w1_scales[a, b][:, cols],
                    rhs=v_words[a][:].bitcast(FP8X4),
                    rhs_scale=v_scales[a][:],
                    start=False,
                    stop=(a == A_PASSES - 1),
                )
            return acc

        def start_sum(n):
            acc = first_product(n, (n - SUM_AHEAD) % RING_BANKS)
            a_sb[n] = after_a(n, [P, S], F32, "a_sb")
            nc.scalar.copy(out=a_sb[n][:], in_=acc[:])
            chunks = S // P
            turned_t[n] = bank(RING_BANKS + n % RING_BANKS, [P, chunks, P])
            for k, term in enumerate((lim_t[n], a_sb[n])):
                for c in range(chunks):
                    nc.tensor.matmul(
                        turned_t[n][:, c, :],
                        term[:, P * c : P * (c + 1)],
                        ident[:],
                        start=(k == 0 and c == 0),
                        stop=(k == 1 and c == chunks - 1),
                        is_transpose=True,
                    )

        def finish_sum(n):
            turned_sb = in_step([P, S // P, P], F32, "turned_sb")
            nc.scalar.activation(out=turned_sb[:], in_=turned_t[n][:], func=ACT.Copy, scale=0.5)
            half_sum[n] = bank(n % RING_BANKS, [P, S // P, P])
            for c in range(S // P):
                nc.tensor.transpose(half_sum[n][:, c, :], turned_sb[:, c, :], ident[:])

        def half_h_tile():
            return keep.tile([P, S], F32, name="h", tag="h")

        def first_half_h():
            h = half_h_tile()
            acc = first_product(0, 0)
            total = in_step([P, S], F32, "total")
            nc.vector.scalar_tensor_tensor(
                out=total[:], in0=acc[:], scalar=0.5, in1=half_lim[:], op0=ALU.mult, op1=ALU.add
            )
            nc.vector.scalar_tensor_tensor(out=h[:], in0=acc[:], scalar=0.0, in1=total[:], op0=ALU.max, op1=ALU.min)
            return h

        def half_h(n):
            h = half_h_tile()
            nc.vector.scalar_tensor_tensor(
                out=h[:],
                in0=a_sb[n][:],
                scalar=0.0,
                in1=half_sum[n][:].rearrange("p c r -> p (c r)"),
                op0=ALU.max,
                op1=ALU.min,
            )
            return h

        def double_wgs(t):
            nc.scalar.mul(out=weight_t[t], in_=weight_t[t], mul=2.0)

        staged, page_bf, x_planes, x_bf, picked = {}, {}, {}, {}, {}
        x_codes, x_scales, page_codes, page_scales = {}, {}, {}, {}

        def scatter(n, h):
            nc.vector.tensor_tensor(
                out=page_t[n][:].indirect(idx2[:]), in0=h[:], in1=weight_t[n % PACK], op=ALU.mult
            )

        def gather(n):
            picked[n] = ring.tile([P, NP], F32, name="picked", bufs=1)
            nc.vector.tensor_copy(out=picked[n][:], in_=page_t[n][:].indirect(idx3[:]))

        def stage(n):
            b, t = divmod(n, PACK)
            if t == 0:
                staged[b] = ring.tile([P, PACK, T2], F32, name="staged", align_bytes=ALIGN)
            nc.sync.dma_start(out=staged[b][:, t, :], in_=page_t[n][:])

        def make_x(n):
            b, t = divmod(n, PACK)
            if n < TILES - X_BEHIND:
                capped = in_step([P, NP], F32, "u")
            else:
                capped = ring.tile([P, NP], F32, name="u_last", tag="lim")
            nc.vector.tensor_scalar(
                out=capped[:],
                in0=picked[n][:],
                scalar1=cen_c[:, b, t : t + 1],
                scalar2=cap_c[:, b, t : t + 1],
                op0=ALU.subtract,
                op1=ALU.min,
            )
            factor = vec_c[:, b, t : t + 1]
            if b < LAST_GROUP:
                if t == 0:
                    x_planes[b] = ring.tile([P, PACK, NP], BF16, name="x_planes")
                nc.scalar.activation(out=x_planes[b][:, t, :], in_=capped[:], func=ACT.Copy, scale=factor)
                return
            if t == 0:
                x_bf[b] = ring.tile([P, NP, PACK], BF16, name="x_last", bufs=1, align_bytes=ALIGN)
            if t < PACK // 2:
                nc.scalar.activation(out=x_bf[b][:, :, t], in_=capped[:], func=ACT.Copy, scale=factor)
            else:
                nc.vector.tensor_scalar(out=x_bf[b][:, :, t], in0=capped[:], scalar1=factor, scalar2=None, op0=ALU.mult)


        def weave_x(b, n):
            x_bf[b] = after_a(n, [P, NP, PACK], BF16, "x_bf")
            nc.scalar.copy(
                out=x_bf[b][:].rearrange("p (c i) t -> p c t i", i=LINE),
                in_=x_planes[b][:].rearrange("p t (c i) -> p c t i", i=LINE),
            )

        def weave_page(b, half, tiles):
            nc.scalar.copy(
                out=page_bf[b, half].rearrange("p (c i) t -> p c t i", i=LINE)[:, :, 0:tiles, :],
                in_=staged[b][:, 0:tiles, HALF * half : HALF * (half + 1)].rearrange("p t (c i) -> p c t i", i=LINE),
            )

        def quant_x(b, buffer):
            x_codes[b] = after_a(buffer, [P, NP], U32, "x_codes")
            x_scales[b] = keep.tile([P, NP], U8, name="x_scales%d" % b, align_bytes=ALIGN)
            nc.vector.quantize_mx(
                out=x_codes[b][:].bitcast(FP8X4), scales=x_scales[b][:], in_=x_bf[b][:].rearrange("p c t -> p (c t)")
            )

        def quant_page(b, half):
            codes = keep.tile([P, HALF], U32, name="page_codes%d_%d" % (b, half), align_bytes=ALIGN)
            scales = keep.tile([P, HALF], U8, name="page_scales%d_%d" % (b, half), align_bytes=ALIGN)
            nc.vector.quantize_mx(
                out=codes[:].bitcast(FP8X4), scales=scales[:], in_=page_bf[b, half].rearrange("p c t -> p (c t)")
            )
            page_codes[b, half], page_scales[b, half] = codes, scales

        page_steps, x_steps = {}, {}
        for b in range(LAST_GROUP):
            first = max(PACK * (b + 1) + 1, LAST_CAST_STEP + 1)
            page_steps[first], page_steps[first + 1] = (b, 0), (b, 1)
            x_steps[first + 2 if first + 2 < LAST_TILE else first] = b

        prepare_w1(0, 0, woven(0, W1_SHAPE, "w1_bf"))
        prepare_last_loaded_w1()
        half_lim = keep.tile([P, S], F32)
        nc.scalar.mul(out=half_lim[:], in_=lim_t[0], mul=0.5)
        double_wgs(0)

        due_t = []
        for n in range(TILES):
            b, t = divmod(n, PACK)
            if n >= X_BEHIND:
                make_x(n - X_BEHIND)
            h = first_half_h() if n == 0 else half_h(n)
            if n >= 1:
                gather(n - 1)
            if n == LAST_TILE:
                quant_x(0, LAST_TILE)
                quant_x(1, 1)
            scatter(n, h)
            if n == 0:
                start_sum(1)
            if n + 1 < PACK:
                double_wgs(n + 1)
            if n + 1 < TILES:
                finish_sum(n + 1)
            if n + SUM_AHEAD < TILES:
                start_sum(n + SUM_AHEAD)
            if n % 2 == 0 and n + LIM_AHEAD < TILES:
                load_lim(n + LIM_AHEAD, nc.scalar)
            if n + PAGE_AHEAD < TILES:
                load_page(n + PAGE_AHEAD)
            if n < A_PASSES:
                load_w1(LAST_GROUP, n, 1)
            if n < LAST_TILE:
                stage(n)
            if b < LAST_GROUP and t < A_PASSES:
                dealt = after_a(0, W1_SHAPE, BF16, "w1_bf") if n == 0 else woven(n, W1_SHAPE, "w1_bf")
                prepare_w1(t, b + 1, dealt)
            if n in page_steps:
                group, half = page_steps[n]
                page_bf[group, half] = woven(n, [P, HALF, PACK], "page_bf")[:]
                weave_page(group, half, PACK)
                quant_page(group, half)
            if n in x_steps:
                weave_x(x_steps[n], n)
            if LAST_CAST_STEP < n <= LAST_CAST_STEP + 2:
                k = n - LAST_CAST_STEP - 1
                due_half = ring.tile([P, M_TILES // 2, NP], F32, name="due", tag="w1_raw", bufs=W1_RAW_BUFS)
                rows = due[HALF * k : HALF * (k + 1), :]
                nc.sync.dma_start(out=due_half[:], in_=rows.rearrange("(i p) j -> p i j", p=P))
                due_t.append(due_half)

        make_x(LAST_TILE - 1)
        gather(LAST_TILE)
        page_last = in_step([P, 2, HALF, PACK], BF16, "page_last")
        for half in range(2):
            page_bf[LAST_GROUP, half] = page_last[:, half]
            weave_page(LAST_GROUP, half, PACK - 1)
        for half in range(2):
            nc.scalar.copy(
                out=page_bf[LAST_GROUP, half][:, :, PACK - 1], in_=page_t[LAST_TILE][:, HALF * half : HALF * (half + 1)]
            )
        make_x(LAST_TILE)
        quant_page(LAST_GROUP, 0)
        quant_x(LAST_GROUP, LAST_GROUP)
        quant_page(LAST_GROUP, 1)

        scores = [bank((m + RING_BANKS) % M_TILES, [P, NP]) for m in range(M_TILES)]
        for b in range(GROUPS):
            for m in range(M_TILES):
                half, c = divmod(m, M_TILES // 2)
                cols = slice(P * c, P * (c + 1))
                nc.tensor.matmul_mx(
                    out=scores[m][:],
                    lhsT=page_codes[b, half][:, cols].bitcast(FP8X4),
                    lhsT_scale=page_scales[b, half][:, cols],
                    rhs=x_codes[b][:].bitcast(FP8X4),
                    rhs_scale=x_scales[b][:],
                    start=(b == 0),
                    stop=(b == LAST_GROUP),
                )
        for m in range(M_TILES):
            half, c = divmod(m, M_TILES // 2)
            diff = after_a(GROUPS + m % Y_BUFS, [P, NP], F32, "y")
            res = ring.tile([P, NP], F32, name="res", tag="page", bufs=PAGE_BUFS)
            pieces = 2 if m == M_TILES - 1 else 1
            for k in range(pieces):
                cols = slice(NP // pieces * k, NP // pieces * (k + 1))
                nc.vector.tensor_tensor(
                    out=diff[:, cols], in0=scores[m][:, cols], in1=due_t[half][:, c, cols], op=ALU.subtract
                )
                nc.scalar.activation(out=res[:, cols], in_=diff[:, cols], func=ACT.Silu)
                nc.sync.dma_start(out=out[P * m : P * (m + 1), cols], in_=res[:, cols])
